import numpy as np, ml_dtypes
CORES = [16,17,18,19,32,33,34,35]
N = 8
BF = ml_dtypes.bfloat16
V, P, L, RO, Q, CAP = 2048, 4096, 224, 2, 2, 48
H, ST = 2048, 9
MS, PO = (7, 7, 8, 9, 10, 11, 12, 14), 20
def rings(rng, hole):
    pool = 1 + np.argsort(rng.random((8, 16, 255)), axis=-1)[..., :PO]
    ms = np.stack([rng.permutation(np.array(MS)) for r in range(N)])
    pal = np.take_along_axis(np.broadcast_to(pool, (N, 8, 16, PO)), np.argsort(rng.random((N, 8, 16, PO)), axis=-1), 3)
    k = np.take_along_axis(pal, (rng.random((N, 8, 16, V)) * ms[:, :, None, None]).astype(np.int64), 3)
    u = rng.random((N, 8, 16, V))
    return np.where(u < hole, 0, np.where(u < hole + 0.05, rng.integers(1, 256, (N, 8, 16, V)), k))
def parts(rng, hole=0.12):
    t = rng.choice(np.array([0, 300, 500, 700, 850]), (N, 8, 16, 1)) + rng.integers(0, 100, (N, 8, 16, 1))
    return rings(rng, hole), rng.integers(0, V, (N, 8, 16, V)), rng.integers(0, 256, (N, 8, 16, P)), rng.integers(0, 256, (N, 8, 16, L)), t
def pack(k, b, x, z, t):
    def bf(a): return np.ascontiguousarray(a.reshape(N, 128, -1)).astype(np.float32).astype(BF)
    return {"ring": bf(k), "nbr": np.ascontiguousarray(b.reshape(N, 128, V)).astype(np.int32), "mat": bf(x), "z0": bf(z), "thr": np.ascontiguousarray(t.reshape(N, 128, 1)).astype(np.int32)}
def setup_inputs(rng):
    return pack(*parts(rng))
def setup_inputs_spread(rng):
    k, b, x, z, t = parts(rng)
    e = rng.integers(5, 13, (N, 8, 1, 1)); ix = np.minimum((255 * rng.random((N, 8, 16, V)) ** e).astype(np.int64), 254)
    keys = 1 + np.argsort(rng.random((8, 16, 255)), axis=-1)
    k = np.take_along_axis(np.broadcast_to(keys, (N, 8, 16, 255)), ix, 3)
    k = np.where(rng.random((N, 8, 16, V)) < rng.random((N, 8, 1, V)) ** 3, 0, k)
    b[:, ::2] = np.minimum((V * rng.random((N, 4, 16, V)) ** 2).astype(np.int64), V - 1)
    x = np.minimum((np.exp2(8 * rng.random((N, 8, 1, P))) * rng.random((N, 8, 16, P))).astype(np.int64), 255)
    z = np.minimum((np.exp2(8 * rng.random((N, 8, 1, L))) * rng.random((N, 8, 16, L))).astype(np.int64), 255)
    t = np.minimum(np.exp2(12 * rng.random((N, 8, 16, 1))).astype(np.int64), 4095)
    return pack(k, b, x, z, t)
def setup_inputs_ends(rng):
    k, b, x, z, t = parts(rng)
    c = rng.random((N, 8, 1, V)); dens = rng.choice(np.array([0.25, 0.25, 0.5]), (N, 8, 1, V))
    k = np.where(c < 0.25, 255, np.where(c < 0.4, 0, np.where(c < 0.85, 255 * (rng.random((N, 8, 16, V)) < dens), k)))
    k[:, 6, :, 2 * ST:ST * (L - 4):ST] = 255
    b = np.where(rng.random((N, 8, 16, V)) < 0.7, (V - 1) * rng.integers(0, 2, (N, 8, 16, V)), b)
    share = np.array([0.5, 0, 0.5, 0, 0, 0, 0, 0]).reshape(8, 1, 1)
    x = np.where(rng.random((N, 8, 1, P)) < share + 0.05, 255 * rng.integers(0, 2, (N, 8, 1, P)), 255 * rng.integers(0, 2, (N, 8, 16, P)))
    z = np.where(rng.random((N, 8, 1, L)) < share, 255 * rng.integers(0, 2, (N, 8, 1, L)), 255 * rng.integers(0, 2, (N, 8, 16, L)))
    t = np.broadcast_to(4095 * (rng.random((1, 8, 16, 1)) < 0.25), (N, 8, 16, 1)); t = np.where(rng.random((N, 8, 16, 1)) < 0.05, 4095 - t, t)
    t[:, 0, 0] = 4095; t[:, 7, 14] = 0; t[:, 7, 15] = 4095
    k[..., V - 1] = 255; k[..., 0] = 255 * (np.argsort(np.argsort(rng.random((N, 8, 16)), axis=-1), axis=-1) < 5)
    x[..., 0] = 0; x[..., P - 1] = 255
    p = np.arange(16)
    for lane in (1, L - 1):
        v = ST * lane; z[..., lane] = 255; k[..., v] = 0; b[:, :, 0, v] = V - 1
        x[..., ((255 * (2 * v + 1) >> 2) + 811 * p) & (P - 1)] = 0 if lane == 1 else 255 * ((p + 1) & 1)
    z[..., 0] = 0; z[..., L - 2] = 0; k[..., ST * (L - 2)] = 0
    a = (15 + Q) >> 1; v = ST * (L - 4); z[..., L - 4] = 0
    k[..., v] = 255 * (p < a); k[..., V - 2] = 255 * (p >= 16 - a); b[:, :, 0, v] = V - 2
    k[..., V - 3] = 255; k[..., V - 4] = 255; b[:, :, 0, V - 2] = V - 2
    for i, u in ((1, V - 1), (14, V - 3), (15, V - 4)): b[:, :, i, V - 2] = u
    return pack(k, b, x, z, t)
def setup_inputs_corners(rng):
    k, b, x, z, t = parts(rng)
    code = rng.integers(1, 256, (N, 8, 16, 1)); code[:, ::2] = code[:1, ::2]; row = np.arange(16)[:, None]
    u = rng.random((N, 8, 1, V))
    k = np.where((row < Q) | (u < 0.33), code, np.where(u < 0.66, rng.integers(1, 256, (N, 8, 16, V)), 0))
    own = np.broadcast_to(np.arange(V), (16, V)); many = (0, 1, CAP - 1, CAP, CAP + 1, L, CAP, L >> 1)
    for r in range(N):
        for g in range(8):
            n = many[(g + r) & 7]; lanes = rng.permutation(L)[:n]; vf = ST * lanes
            if g & 3 == 1: b[r, g] = np.where(rng.random((16, V)) < 0.5, own, b[r, g])
            if g & 3 == 2: b[r, g] = np.where(rng.random((16, V)) < 0.3, (V - 1) * rng.integers(0, 2, (16, V)), b[r, g])
            if g & 3 == 3: b[r, g] = np.where(rng.random((16, V)) < 0.5, rng.integers(0, V, (1, V)), b[r, g])
            gone = np.zeros(V, bool); gone[vf] = True
            b[r, g] = b[r, g] + gone[b[r, g]]
            if g & 3 == 1: b[r, g][:, vf[::2]] = vf[::2]
            k[r, g][:, vf] = np.where((row < Q - 1) & (rng.random(n) < 0.5), code[r, g], 0)
    t = np.where(rng.random((N, 8, 16, 1)) < 0.5, rng.choice(np.array([0, 1, 15, 600, 1000, 4095]), (N, 8, 16, 1)), t); t[:, ::2, :Q] = 0; t[:, 1, 15] = 4095
    x = np.where(rng.random((N, 8, 1, P)) < 0.2, rng.choice(np.array([0, 128, 255]), (N, 8, 1, P)), x)
    z = np.where(rng.random((N, 8, 1, L)) < 0.3, rng.choice(np.array([0, 1, 254, 255]), (N, 8, 1, L)), z)
    return pack(k, b, x, z, t)
def setup_inputs_crowd(rng):
    k, b, x, z, t = parts(rng, 0.22)
    k = np.where(rng.random((N, 8, 1, V)) < 0.03, 0, k)
    hubs = np.argsort(rng.random((N, 8, V)), axis=-1)[..., :12]
    h = np.take_along_axis(hubs, rng.integers(0, 12, (N, 8, 16 * V)), 2).reshape(N, 8, 16, V)
    b = np.where(rng.random((N, 8, 16, V)) < 0.6, h, b)
    x[:, 1::2] = np.take_along_axis(x[:, 1::2], np.broadcast_to(rng.integers(0, 8, (N, 4, 1, P)), (N, 4, 16, P)), 3)
    z[..., 1::2] = z[..., ::2]
    return pack(k, b, x, z, t)
def setup_inputs_far(rng):
    k, b, x, z, t = parts(rng); a = (15 + Q) >> 1; kk = np.arange(16)[:, None]
    up = rng.integers(0, 2, (N, 8, 1, 1)); up[0, 0] = 0; up[N - 1, 7] = 1
    x = rng.integers(0, 48, (N, 8, 16, P)) + 208 * up; z = rng.integers(0, 48, (N, 8, 16, L)) + 208 * (1 - up)
    t = np.where(rng.random((N, 8, 16, 1)) < 0.4, rng.integers(3000, 3500, (N, 8, 16, 1)), t)
    first = ST * np.arange(L); rest = np.setdiff1d(np.arange(V), first)
    for r in range(N):
        for g in range(8):
            if (g + r) & 1: continue
            code = rng.integers(1, 256, (16, 1)); o = rng.permutation(16)[:, None]
            rare = 1 + (code - 1 + rng.integers(1, 255, (16, V))) % 255
            other = np.where(rng.random((16, V)) < 0.7, 0, rare)
            u = rng.permutation(rest); q = len(u) >> 2; near = u[:q]; full = u[q:2 * q]; right = u[2 * q:3 * q]
            kr = k[r, g]; br = b[r, g]
            kr[:, first] = np.where(o < a, code, other[:, first])
            kr[:, right] = np.where(o >= 16 - a, code, other[:, right])
            kr[:, full] = code
            kr[:, near] = np.where(o == rng.integers(a, 16, q), rare[:, near], code)
            e = ST * rng.permutation(L)[:L >> 4]
            kr[:, e[::2]] = 0; kr[:, e[1::2]] = code
            br[:, first] = rng.choice(right, (16, L))
            i = rng.integers(0, 15, q); m = i + 1 + (rng.random(q) * (15 - i)).astype(np.int64)
            pick = rng.random((16, q)); low = rng.choice(near, (16, q)); top = rng.choice(full, (16, q)); poor = rng.choice(np.concatenate([first, u[2 * q:]]), (16, q))
            late = np.where((kk == m) | (pick < 0.4), top, np.where(pick < 0.7, low, poor))
            early = np.where((kk == i) | ((kk > i) & (pick < 0.5)), low, poor)
            br[:, right] = np.where(kk < m, early, late)
    return pack(k, b, x, z, t)
def check_inputs(d):
    bad = []
    for k, lo, hi in (("ring", 0, 255), ("nbr", 0, V - 1), ("mat", 0, 255), ("z0", 0, 255), ("thr", 0, 4095)):
        a = np.asarray(d[k]).astype(np.float64)
        if not (np.min(a) >= lo and np.max(a) <= hi): bad.append("range of " + k)
        elif np.any(a != np.floor(a)): bad.append("whole numbers in " + k)
    return bad
def columns(a, ix):
    return np.take_along_axis(a, ix[:, :, None, :], 3)
def by_lane(a):
    return np.ascontiguousarray(a.transpose(0, 1, 3, 2)).reshape(N, 8, L * 16)
def reference(ring, nbr, mat, z0, thr):
    K = ring.astype(np.float32).astype(np.int64).reshape(N, 8, 16, V); B = nbr.astype(np.int64).reshape(N, 8, 16, V)
    X = mat.astype(np.float32).astype(np.int64).reshape(N, 8, 16, P); z = z0.astype(np.float32).astype(np.int64).reshape(N, 8, 16, L)
    th = thr.astype(np.int64).reshape(N, 8, 16, 1); v = np.array(np.broadcast_to(ST * np.arange(L), (N, 8, L)))
    failures = np.zeros(N, np.int64); rv_old = np.zeros((N, 8, 16), np.int64); row = np.arange(16)[:, None]
    for t in range(RO):
        j = (np.sum(z, axis=2) + t) & 15
        n = np.take_along_axis(columns(B, v), j[:, :, None, :], 2)[:, :, 0]
        Kv = columns(K, v); Kn = columns(K, n)
        direct = np.sum((Kv == Kn) & (Kv > 0), axis=2) >= Q
        cand = by_lane(columns(B, n)); Kc = columns(K, cand).reshape(N, 8, 16, L, 16)
        score = np.minimum(np.sum((Kc == Kv[..., None]) & (Kc > 0), axis=2), np.sum((Kc == Kn[..., None]) & (Kc > 0), axis=2))
        k = np.argmax(score, axis=3)
        bridged = ~direct & (np.max(score, axis=3) >= Q); failed = ~direct & ~bridged
        w = np.where(bridged, np.take_along_axis(cand.reshape(N, 8, L, 16), k[..., None], 3)[..., 0], n)
        Kw = columns(K, w)
        place = (((Kw * (2 * v + 1)[:, :, None, :]) >> 2) + 811 * row + t) & (P - 1)
        Xc = columns(X, by_lane(place)).reshape(N, 8, 16, L, 16)
        d = np.sum(np.abs(Xc - z[..., None]), axis=2)
        p = np.argmin(d, axis=3)
        x = np.take_along_axis(Xc, p[:, :, None, :, None], 4)[..., 0]
        caught = (d.transpose(0, 1, 3, 2) < th + (failures & 15)[:, None, None, None]) & (Kw > 0)
        low = np.argmax(caught, axis=3)
        rv = np.where(np.any(caught, axis=3), np.take_along_axis(Kw, low[..., None], 3)[..., 0], 0)
        fi = failed.astype(np.int64); served = failed & (np.add.accumulate(fi, axis=2) - fi < CAP)
        h = np.sum(Kw * z, axis=2) & (H - 1)
        given = columns(np.roll(K, -1, axis=0), h)
        filled = np.where(Kv > 0, Kv, np.where(bridged[:, :, None, :], Kw, given))
        K2 = np.array(K); B2 = np.array(B); active = bridged | served
        for a in range(N):
            for g in range(8):
                i = np.nonzero(active[a, g])[0]
                u, first = np.unique(v[a, g, i], return_index=True); i = i[first]
                K2[a, g][:, u] = filled[a, g][:, i]
                i = i[bridged[a, g, i]]; B2[a, g, j[a, g, i], v[a, g, i]] = w[a, g, i]
        come = np.roll(rv_old, 1, axis=0)
        K = np.where((K2 == rv[..., None]) | (K2 == come[..., None]), 0, K2); B = B2
        z = (z + x) >> 1; v = w; rv_old = rv; failures = np.sum(fi, axis=(1, 2))
    return {"yk": K.reshape(N, 128, V).astype(np.float32).astype(BF), "yz": z.reshape(N, 128, L).astype(np.float32)}

@@ -1,0 +1,549 @@
+from concourse.mybir import AluOpType as ALU, AxisListType, ActivationFunctionType as AF
+
+L, V = 224, 2048
+CH = [(0, 128), (128, 224)]
+BASE = [0, 17 * 128]
+NXT = 17 * 224
+SCRATCH, SMALL = {}, {}
+for _n, _w, _d in (
+        ("ringS", V + L, "bfloat16"), ("nbrS", V + L, "int32"), ("matS", 4096, "bfloat16"), ("thrI", 1, "int32"),
+        ("num", V + L, "float32"), ("BIG0", NXT + V, "bfloat16"), ("BIG1", NXT + V, "bfloat16"),
+        ("zb0", L, "bfloat16"), ("zb1", L, "bfloat16"), ("zf", L, "float32"), ("XC0", 2048, "bfloat16"), ("XC1", 1536, "bfloat16"),
+        ("ones", 256, "bfloat16"), ("sel1", 144, "bfloat16"), ("selk", 144, "bfloat16"), ("selm", 144, "bfloat16"),
+        ("blk", 128, "bfloat16"), ("blkz", 128, "bfloat16"), ("blkf", 128, "float32"), ("trid", 128, "bfloat16"),
+        ("idn", 128, "bfloat16"), ("nidn", 128, "bfloat16"), ("l16", 128, "bfloat16"), ("cn", L, "bfloat16"), ("chh", L, "bfloat16"),
+        ("rowA", 128, "bfloat16"), ("rowB", 128, "bfloat16"), ("rneg", L, "float32"), ("rmul", L, "float32"), ("ramp", L, "bfloat16"),
+        ("tri", L, "bfloat16"), ("zer", 16, "float32"), ("pI", 1, "int32"), ("qI", 1, "int32"), ("qc", 1, "float32"),
+        ("pc0", 1, "float32"), ("pc1", 1, "float32"), ("tp0", 1, "float32"), ("tp1", 1, "float32"), ("pk", 1, "float32"),
+        ("thr0", 1, "float32"), ("thr1", 1, "float32"), ("tmpc", 1, "float32"), ("rowc", 16, "float32"),
+        ("iW", 14, "float32"), ("nk", 14, "float32"), ("dW", 14, "float32"), ("cb", 14, "float32"), ("vW0", 14, "float32"),
+        ("vW1", 14, "float32"), ("V20", L, "float32"), ("V21", L, "float32"),
+        ("JI", L, "int32"), ("JM", L, "int32"), ("YY", L, "float32"), ("SW", L, "float32"), ("nW", 14, "float32"),
+        ("noff", 14, "uint16"), ("Bn", L, "uint16"), ("BnF", L, "float32"), ("BvT", L, "int32"), ("KvT", L, "bfloat16"),
+        ("hv", L, "bfloat16"), ("hn", L, "bfloat16"), ("E3", L, "bfloat16"),
+        ("M2", 128, "float32"), ("MM", 128, "float32"), ("SK", L, "float32"), ("SD", L, "float32"),
+        ("posU", 14, "uint16"), ("KI", 14, "int32"), ("KA", 14, "int32"), ("KK", 14, "int32"), ("xn", 14, "float32"),
+        ("bb", 14, "float32"), ("nb", 14, "float32"), ("nd", 14, "float32"), ("PR", 128, "float32"), ("PI", 128, "int32"),
+        ("PJ", 128, "int32"), ("PL", L, "uint16"), ("KwT", L, "bfloat16"), ("DI", 14, "int32"), ("DA", 14, "int32"),
+        ("pxU", 14, "uint16"), ("ZS", 128, "float32"), ("ZI", 128, "int32"),
+        ("NZ", L, "bfloat16"), ("N1", L, "bfloat16"), ("cap", L, "float32"), ("com", L, "float32"), ("rvc", 1, "float32"),
+        ("rvi", 1, "int32"), ("rvj", 1, "int32"), ("rv0", 4, "float32"), ("rv1", 4, "float32"), ("come", 4, "float32"), ("HZ", L, "float32"),
+        ("SH", L, "float32"), ("HI", 14, "int32"), ("HJ", 14, "int32"), ("FF", 14, "bfloat16"), ("Finc", 14, "bfloat16"),
+        ("srv", 14, "float32"), ("th", 14, "float32"), ("sp", 14, "float32"), ("spU", 14, "uint16"),
+        ("SRC", L, "bfloat16"), ("FP", L, "bfloat16"), ("ta", 14, "float32"), ("oKf", 14, "float32"), ("oKU", 28, "uint16"),
+        ("oBU", 14, "uint16"), ("oB2", 14, "float32"), ("cdU", 14, "uint16"), ("cdR", L, "float32"), ("mk", L, "float32"), ("SV", L, "float32"),
+        ("voff", 14, "uint16"), ("wR", L, "float32"), ("Bm", L, "float32"), ("Bs", L, "float32"), ("Bx", L, "int32"),
+        ("fc", 1, "float32"), ("fi", 1, "int32"), ("fj", 1, "int32"),
+        ("rpI", L, "int32"), ("rp", 14, "uint16"), ("vh", L, "float32"), ("va", L, "float32"), ("eq", L, "float32"), ("SE", L, "float32"),
+        ("e0", V, "bfloat16"), ("e1", V, "bfloat16"), ("ykS", V, "bfloat16"), ("vWp", 16, "float32")):
+    if _w in (1, 14) and _d != "uint16" and _n not in ("thrI", "FF", "Finc"):
+        _b = "small" + _d
+        SMALL[_n] = (_b, 16 * len(SMALL), _w)
+        SCRATCH[_b] = ("sbuf", [128, 16 * len(SMALL)], _d)
+    else:
+        SCRATCH[_n] = ("sbuf", [128, _w], _d)
+for _n in ("E1", "E2", "DD"):
+    SCRATCH[_n] = ("sbuf", [128, L, 16], "bfloat16")
+BANKS = ("PZ", "PK", "PC0", "PC1", "PD0", "PD1", "PA", "PM")
+for _n in BANKS:
+    SCRATCH[_n] = ("psum", [128, 512], "float32")
+SEMAPHORES = ["sV", "sS", "sP", "sG", "xr0", "xr1", "xl0", "xl1", "rr", "rl"] + ["d%d" % i for i in range(16)]
+
+
+def rank_program(g, core, T, topo):
+    rank = T.rank_of(core)
+    if rank is None:
+        return
+    N = len(T.cores)
+    queue = {"V": g.vector, "S": g.scalar, "P": g.tensor, "G": g, "Y": g.sync}
+    semof = {"V": "sV", "S": "sS", "P": "sP", "G": "sG"}
+    total = {}
+    known = {e: {} for e in queue}
+    log = {}
+
+    def need(e, refs, write):
+        out = []
+        for name, lo, hi, tag in refs:
+            for (l2, h2, w2, e2, s2, c2, k2, t2) in log.get(name, ()):
+                if name in BANKS:
+                    if e2 == e and (write or not w2):
+                        continue
+                else:
+                    if not (l2 < hi and lo < h2) or not (write or w2):
+                        continue
+                    if tag and t2 and tag[0] == t2[0] and tag[1] != t2[1]:
+                        continue
+                    if e2 == e and s2 == semof.get(e) and not w2:
+                        continue
+                out.append((s2, c2, k2))
+        return out
+
+    def note(e, refs, write, s, c, snap):
+        for name, lo, hi, tag in refs:
+            acc = log.setdefault(name, [])
+            if name in BANKS:
+                acc[:] = [a for a in acc if not (a[3] == e and a[2] == write)]
+            elif write:
+                acc[:] = [a for a in acc if not (lo <= a[0] and a[1] <= hi and tag in (None, a[7]))]
+            else:
+                acc[:] = [a for a in acc if a[2] or not (a[3] == e and a[4] == s and lo <= a[0] and a[1] <= hi and tag in (None, a[7]))]
+            acc.append((lo, hi, write, e, s, c, snap, tag))
+
+    def waits(e, deps):
+        todo = {}
+        for s, c, k in deps:
+            if known[e].get(s, 0) < c and todo.get(s, (0,))[0] < c:
+                todo[s] = (c, k)
+        for s in list(todo):
+            c = todo[s][0]
+            if any(o != s and todo[o][1].get(s, 0) >= c for o in todo):
+                del todo[s]
+        for s, (c, k) in todo.items():
+            queue[e].wait_ge(T.sem[s], c)
+            for a, b in k.items():
+                known[e][a] = max(known[e].get(a, 0), b)
+            known[e][s] = max(known[e].get(s, 0), c)
+
+    def emit(e, fn, reads, writes, sem=None, inc=1):
+        s = sem or semof[e]
+        rd = [r[1:] for r in reads]
+        wr = [r[1:] for r in writes]
+        waits(e, need(e, rd, False) + need(e, wr, True))
+        fn().then_inc(T.sem[s], inc)
+        total[s] = total.get(s, 0) + inc
+        snap = dict(known[e])
+        snap[s] = total[s]
+        note(e, rd, False, s, total[s], snap)
+        note(e, wr, True, s, total[s], snap)
+
+    def R(name, lo=0, hi=None, step=1, p=None):
+        if name in SMALL:
+            name, off, w = SMALL[name]
+            lo, hi = lo + off, off + (w if hi is None else hi)
+        hi = T[name].shape[1] if hi is None else hi
+        ps = slice(None) if p is None else slice(0, p)
+        ap = T[name][ps, lo:hi] if step == 1 else T[name][ps, lo:hi:step]
+        return (ap, name, lo, hi, None if step == 1 else (step, lo % step))
+
+    def X(name, lo, hi, off):
+        return (T[name][:, lo:hi].indirect(off[0]), name, lo, hi, None)
+
+    def E3d(name, l0, l1, k=None, q=None):
+        ap = T[name][:, l0:l1, k] if k is not None else T[name][:, l0 + q:l1:16, :]
+        return (ap, name, l0, l1, ("q", q) if k is None else ("k", k))
+
+    def cols(*xs):
+        return [x for x in xs if isinstance(x, tuple)]
+
+    def val(x):
+        return x[0] if isinstance(x, tuple) else x
+
+    def ts(out, a, s1, s2, op0, op1=None):
+        rd = [a] + cols(s1, s2)
+        if op1 is None:
+            emit("V", lambda: g.vector.tensor_scalar(out[0], a[0], val(s1), None, op0), rd, [out])
+        else:
+            emit("V", lambda: g.vector.tensor_scalar(out[0], a[0], val(s1), val(s2), op0, op1), rd, [out])
+
+    def tt(out, a, b, op, off=()):
+        emit("V", lambda: g.vector.tensor_tensor(out[0], a[0], b[0], op), [a, b] + list(off), [out])
+
+    def cp(out, a, off=()):
+        emit("V", lambda: g.vector.tensor_copy(out[0], a[0]), [a] + list(off), [out])
+
+    def scan(out, d0, d1, op0, op1):
+        emit("V", lambda: g.vector.tensor_tensor_scan(out[0], d0[0], d1[0], 0.0, op0, op1), [d0, d1], [out])
+
+    def red(out, a, op):
+        emit("V", lambda: g.vector.tensor_reduce(out[0], a[0], AxisListType.X, op), [a], [out])
+
+    def ac(out, a, func=AF.Copy, off=(), **kw):
+        emit("S", lambda: g.scalar.activation(out[0], a[0], func, **kw), [a] + list(off), [out])
+
+    def fill(out, c):
+        emit("V", lambda: g.vector.memset(out[0], c), [], [out])
+
+    def mm(out, lhsT, rhs, start, stop):
+        emit("P", lambda: g.tensor.matmul(out[0], lhsT[0], rhs[0], start, stop), [lhsT, rhs], [out])
+
+    def iota(out, pattern, base, cm):
+        emit("G", lambda: g.iota(out[0], pattern, base, cm, allow_small_or_imprecise_dtypes=True), [], [out])
+
+    def asel(out, a, pattern, op, fillv, base, cm):
+        emit("G", lambda: g.affine_select(out[0], a[0], pattern, op, fillv, base, cm), [a], [out])
+
+    ndma = [0]
+
+    def dma(e, out, a, rd=(), wr=()):
+        s = "d%d" % ndma[0]
+        ndma[0] += 1
+        emit(e, lambda: queue[e].dma_start(out, a), list(rd), list(wr), s, 16)
+
+    def remote(out_ap, src, rsem, lsem, dst):
+        rid, pid, _ = topo.addr(dst)
+        n = len(topo.engines(core, dst))
+        waits("G", need("G", [src[1:]], False))
+        g.remote_dma(out_ap, src[0], T.sem[rsem], T.sem[lsem], pid, rid, topo.mask(core, dst))
+        total[lsem] = total.get(lsem, 0) + n
+        snap = dict(known["G"])
+        snap[lsem] = total[lsem]
+        note("G", [src[1:]], False, lsem, total[lsem], snap)
+
+    def landed(name, lo, hi, rsem, src):
+        n = len(topo.engines(src, core))
+        total[rsem] = total.get(rsem, 0) + n
+        note("R", [(name, lo, hi, None)], True, rsem, total[rsem], {rsem: total[rsem]})
+
+    prev, nxt = T.cores[(rank - 1) % N], T.cores[(rank + 1) % N]
+    dma("Y", T.zb0[:, :], T.z0[:, :], wr=[R("zb0")])
+    dma("Y", T.nbrS[:, 0:V], T.nbr[:, :], wr=[R("nbrS", 0, V)])
+    dma("S", T.ringS[:, 0:V], T.ring[:, :], wr=[R("ringS", 0, V)])
+    dma("S", T.thrI[:, :], T.thr[:, :], wr=[R("thrI")])
+    dma("Y", T.matS[:, :], T.mat[:, :], wr=[R("matS")])
+    fill(R("ones"), 1.0)
+    fill(R("sel1"), 0.0)
+    fill(R("sel1", 15, 143, 16), 1.0)
+    iota(R("pI"), [[1, 1]], 0, 1)
+    o8 = R("ones", 0, 128)
+    asel(R("blk"), o8, [[-16, 8], [0, 16]], ALU.is_ge, 0.0, 0, 1)
+    asel(R("blk"), R("blk"), [[16, 8], [0, 16]], ALU.is_ge, 0.0, 15, -1)
+    asel(R("idn"), o8, [[-1, 128]], ALU.is_equal, 0.0, 0, 1)
+    asel(R("l16", p=16), R("ones", 0, 128, p=16), [[0, 8], [-1, 16]], ALU.is_equal, 0.0, 0, 1)
+    asel(R("cn", p=16), R("ones", 0, L, p=16), [[0, 14], [-1, 16]], ALU.is_equal, 0.0, 0, 1)
+    s8 = R("sel1", 15, 143, 16)
+    asel(s8, s8, [[-16, 8]], ALU.is_ge, 0.0, 0, 1)
+    asel(s8, s8, [[16, 8]], ALU.is_ge, 0.0, 15, -1)
+    iota(R("rowA"), [[-256, 8], [0, 16]], 1792, 0)
+    iota(R("rowB"), [[0, 8], [-1, 16]], 255, -16)
+    iota(R("rowc", 0, 14), [[16, 14]], 0, 0)
+    iota(R("V20"), [[18, L]], 1, 0)
+    iota(R("ramp"), [[-256, L]], 256 * L, 0)
+    asel(R("trid"), R("blk"), [[-1, 128]], ALU.is_gt, 0.0, 0, 1)
+    iota(R("rpI"), [[1, 14], [0, 16]], 0, 0)
+    iota(R("vh"), [[0, 14], [1, 16]], 0, 0)
+    iota(R("num"), [[1, V + L]], 0, 0)
+    ts(R("qI"), R("pI"), 15, None, ALU.bitwise_and)
+    cp(R("qc"), R("qI"))
+    for t in range(2):
+        ts(R("pc%d" % t), R("qc"), 811.0, t - 0.375, ALU.mult, ALU.add)
+        ts(R("tp%d" % t), R("qc"), -2048.0, 2048.0 * (16 + t), ALU.mult, ALU.add)
+    ts(R("pk"), R("qc"), -1.0, 16.0, ALU.mult, ALU.add)
+    fill(R("rneg"), 0.0)
+    fill(R("rneg", 0, L, 16), -float(1 << 24))
+    fill(R("zer"), 0.0)
+    fill(R("rmul"), 1.0)
+    fill(R("rmul", 0, L, 16), 0.0)
+    ts(R("blkz"), R("blk"), 2048.0, None, ALU.mult)
+    cp(R("blkf"), R("blk"))
+    ts(R("chh", p=16), R("cn", p=16), float(1 << 21), -float(1 << 21), ALU.mult, ALU.add)
+    ts(R("cn", p=16), R("cn", p=16), float((1 << 20) - 2048 * 120), -float(1 << 20), ALU.mult, ALU.add)
+    ts(R("selk", 0, 143), R("sel1", 0, 143), 4096.0, None, ALU.mult)
+    ts(R("selm", 0, 143), R("sel1", 0, 143), -2048.0, None, ALU.mult)
+    ts(R("nidn"), R("idn"), -1.0, None, ALU.mult)
+    ts(R("iW"), R("rowc", 0, 14), R("qc"), None, ALU.add)
+    for h, (l0, l1) in enumerate(CH):
+        a, b = l0 // 16, l1 // 16
+        nl = l1 - l0
+        ts(R("nk", a, b), R("iW", a, b), -1.0, float(4096 + 2047 + nl + l0), ALU.mult, ALU.add)
+        fill(R("cb", a, b), float(BASE[h] + 2047 + nl))
+    ts(R("dW"), R("iW"), float(V), None, ALU.add)
+    ts(R("vW0"), R("iW"), 9.0, None, ALU.mult)
+
+    def late_constants():
+        ts(R("trid"), R("trid"), -1.0, None, ALU.mult)
+        ts(R("tri"), R("vh"), R("qc"), None, ALU.is_lt)
+        cp(R("rp"), R("rpI", 0, L, 16))
+        cp(R("thr0"), R("thrI"))
+
+    def sel(name, q):
+        return R(name, 15 - q, 143 - q)
+
+    def low(P, nl, last=False):
+        mm(P, R("ones", 0, 128, p=1), R("rowA", 0, nl, p=1), True, False)
+        mm(P, R("l16", p=16), R("rowB", 0, nl, p=16), False, False)
+
+    def revoke(t, rv, out, banks):
+        for m in range(4):
+            a, b = 512 * m, 512 * m + 512
+            P = R(banks[m])
+            mm(P, R("idn"), R("ringS", a, b), True, False)
+            if t == 1:
+                mm(P, R("nidn"), R("e1", a, b), False, False)
+        for m in range(4):
+            a, b = 512 * m, 512 * m + 512
+            ts(R("e0", a, b), R("ringS", a, b), rv, rv, ALU.is_equal, ALU.mult)
+            mm(R(banks[m]), R("nidn"), R("e0", a, b), False, True)
+        for m in range(4):
+            a, b = 512 * m, 512 * m + 512
+            if t == 0 or m % 2 == 0:
+                ac(R(out, a, b), R(banks[m]))
+            else:
+                cp(R(out, a, b), R(banks[m]))
+            if t == 1:
+                dma("Y" if m % 2 else "S", T.yk[:, a:b], T[out][:, a:b], rd=[R(out, a, b)])
+
+    def step1(t):
+        zb = R("zb%d" % t)
+        mm(R("PZ", 0, L), R("blkz"), zb, True, True)
+        mm(R("PM", 0, L), R("idn"), zb, True, True)
+        ts(R("JI"), R("PZ", 0, L), R("tp%d" % t), None, ALU.add)
+        ts(R("JM"), R("JI"), 15 * 2048, None, ALU.bitwise_and)
+        tt(R("YY"), R("JM"), R("nbrS", 0, 2008, 9) if t == 0 else R("BvT"), ALU.max)
+        mm(R("PZ", 0, L), R("l16", p=16), R("cn", p=16), True, False)
+        mm(R("PZ", 0, L), R("blkf"), R("YY"), False, True)
+        scan(R("SW"), R("rneg"), R("PZ", 0, L), ALU.add, ALU.max)
+        cp(R("noff"), R("SW", 15, L, 16))
+
+    for t in range(2):
+        zb, V2, vW, BIG = "zb%d" % t, "V2%d" % t, "vW%d" % t, "BIG%d" % t
+        if t == 0:
+            remote(T.BIG0[:, NXT:NXT + V], R("ringS", 0, V), "xr0", "xl0", prev)
+            ac(R("KvT"), R("ringS", 0, 2008, 9))
+            step1(0)
+        ts(R("hv"), R("KvT"), 0.0, None, ALU.is_equal)
+        mm(R("PK", 0, L), R("idn"), R("KvT"), True, False)
+        mm(R("PK", 0, L), R("nidn"), R("hv"), False, True)
+        for h, (l0, l1) in enumerate(CH):
+            a, b, nl = l0 // 16, l1 // 16, l1 - l0
+            no = R("noff", a, b)
+            cp(R("Bn", l0, l1), X("nbrS", 0, V, no), off=[no])
+            ac(R(BIG, BASE[h], BASE[h] + nl), X("ringS", 0, V, no), off=[no])
+
+        def gk(h, a, b):
+            l0, l1 = CH[h]
+            lo = BASE[h] + (l1 - l0) + 16 * (a - l0)
+            o = R("Bn", a, b)
+            ac(R(BIG, lo, lo + 16 * (b - a)), X("ringS", 0, V, o), off=[o])
+
+        gk(0, 0, 64)
+        gk(0, 64, 128)
+        gk(1, 128, 224)
+        for h, (l0, l1) in enumerate(CH):
+            nl = l1 - l0
+            ts(R("hn", l0, l1), R(BIG, BASE[h], BASE[h] + nl), 0.0, None, ALU.is_equal)
+            P = R("PK", L + l0, L + l1)
+            mm(P, R("idn"), R(BIG, BASE[h], BASE[h] + nl), True, False)
+            mm(P, R("nidn"), R("hn", l0, l1), False, True)
+        for h, (l0, l1) in enumerate(CH):
+            tt(R("E3", l0, l1), R("PK", l0, l1), R(BIG, BASE[h], BASE[h] + l1 - l0), ALU.is_equal)
+        if t == 0:
+            late_constants()
+
+        def compare(h, which, parts):
+            l0, l1 = CH[h]
+            nl, nc = l1 - l0, (l1 - l0) // 16
+            En, ko = ("E1", 0) if which == 0 else ("E2", L)
+            for a, b in parts:
+                lo = BASE[h] + nl + 16 * (a - l0)
+                for k in range(16):
+                    tt(E3d(En, a, b, k=k), R("PK", ko + a, ko + b), R(BIG, lo + k, lo + 16 * (b - a), 16), ALU.is_equal)
+            if which == 0:
+                P = R("PC%d" % h, 2 * nl, 2 * nl + nc)
+                for q in range(16):
+                    mm(P, sel("sel1", q), R("E3", l0 + q, l1, 16), q == 0, q == 15)
+            P = R("PC%d" % h, which * nl, (which + 1) * nl)
+            low(P, nl)
+            for q in range(16):
+                mm(P, sel("selk", q), E3d(En, l0, l1, q=q), False, q == 15)
+
+        def tail(h):
+            l0, l1 = CH[h]
+            a, b, nl, nc = l0 // 16, l1 // 16, l1 - l0, (l1 - l0) // 16
+            PC = "PC%d" % h
+            cp(R("M2", 0, nl), R(PC, nl, 2 * nl))
+            ts(R("xn", a, b), R(PC, 2 * nl, 2 * nl + nc), 2.0, float(1 << 18), ALU.is_ge, ALU.mult)
+            tt(R("MM", 0, nl), R(PC, 0, nl), R("M2", 0, nl), ALU.min)
+            tt(R("xn", a, b), R("xn", a, b), R("nk", a, b), ALU.add)
+            scan(R("SK", l0, l1), R("rneg", 0, nl), R("MM", 0, nl), ALU.add, ALU.max)
+            tt(R("KI", a, b), R("SK", l0 + 15, l1, 16), R("xn", a, b), ALU.max)
+            ts(R("KA", a, b), R("KI", a, b), 4095, None, ALU.bitwise_and)
+            po = R("posU", a, b)
+            ts(po, R("KA", a, b), -1.0, float(2047 + nl), ALU.mult, ALU.add)
+            w = X(BIG, BASE[h], BASE[h] + 17 * nl, po)
+            tt(R("PR", 0, nl), w, R(V2, l0, l1), ALU.mult, off=[po])
+            ac(R("KwT", l0, l1), w, off=[po])
+            ts(R("PI", 0, nl), R("PR", 0, nl), 0.25, R("pc%d" % t), ALU.mult, ALU.add)
+            ts(R("PJ", 0, nl), R("PI", 0, nl), 4095, None, ALU.bitwise_and)
+            cp(R("PL", l0, l1), R("PJ", 0, nl))
+
+        def gx(h):
+            l0, l1 = CH[h]
+            o = R("PL", l0, l1)
+            ac(R("XC%d" % h), X("matS", 0, 4096, o), off=[o])
+
+        def dsub(h, m):
+            l0, l1 = CH[h]
+            nl = l1 - l0
+            bank = ("PC0", "PK", "PC1")[(4 * h + m) % 3]
+            for p in range(4 * m, 4 * m + 4):
+                P = R(bank, (p & 3) * 128, (p & 3) * 128 + nl)
+                mm(P, R("nidn"), R(zb, l0, l1), True, False)
+                mm(P, R("idn"), R("XC%d" % h, p, 16 * nl, 16), False, True)
+            for p in range(4 * m, 4 * m + 4):
+                ac(E3d("DD", l0, l1, k=p), R(bank, (p & 3) * 128, (p & 3) * 128 + nl), AF.Abs)
+
+        def dW(h, m):
+            l0, l1 = CH[h]
+            P = R("PD%d" % h, 0, l1 - l0)
+            if m == 0:
+                low(P, l1 - l0)
+            for q in range(4 * m, 4 * m + 4):
+                mm(P, sel("selm", q), E3d("DD", l0, l1, q=q), False, q == 15)
+
+        def dA(h, m):
+            l0, l1 = CH[h]
+            for p in range(4 * m, 4 * m + 4):
+                mm(R("PA", l0, l1), sel("sel1", p), E3d("DD", l0, l1, k=p), p == 0, p == 15)
+
+        def best(h):
+            l0, l1 = CH[h]
+            a, b, nl = l0 // 16, l1 // 16, l1 - l0
+            scan(R("SD", l0, l1), R("rneg", 0, nl), R("PD%d" % h, 0, nl), ALU.add, ALU.max)
+            cp(R("DI", a, b), R("SD", l0 + 15, l1, 16))
+            ts(R("DA", a, b), R("DI", a, b), 2047, None, ALU.bitwise_and)
+            po = R("pxU", a, b)
+            ts(po, R("DA", a, b), -1.0, 2047.0, ALU.mult, ALU.add)
+            tt(R("ZS", 0, nl), X("XC%d" % h, 0, 16 * nl, po), R(zb, l0, l1), ALU.add, off=[po])
+            ts(R("ZI", 0, nl), R("ZS", 0, nl), 0.5, -0.25, ALU.mult, ALU.add)
+            cp(R("zb1" if t == 0 else "zf", l0, l1), R("ZI", 0, nl))
+
+        compare(0, 0, [(0, 64), (64, 128)])
+        compare(0, 1, [(0, 128)])
+        compare(1, 0, [(128, 224)])
+        tail(0)
+        gx(0)
+        compare(1, 1, [(128, 224)])
+        tail(1)
+        gx(1)
+        ts(R("FF"), R("KI"), 8192.0, None, ALU.is_lt)
+        emit("V", lambda: g.vector.tensor_tensor_scan(T.Finc[:, :], T.FF[:, :], T.zer[:, 0:14], 0.0, ALU.add, ALU.add), [R("FF"), R("zer", 0, 14)], [R("Finc")])
+        mm(R("PZ", 224, 238), R("blk"), R("Finc"), True, False)
+        mm(R("PZ", 224, 238), R("trid"), R("FF"), False, True)
+        if t == 0:
+            mm(R("PZ", 240, 254), R("ones", 0, 128), R("FF"), True, True)
+        tt(R("HZ"), R("PM", 0, L), R("KwT"), ALU.mult)
+        mm(R("PZ", 0, L), R("l16", p=16), R("chh", p=16), True, False)
+        mm(R("PZ", 0, L), R("blkf"), R("HZ"), False, True)
+        ts(R("nd"), R("KI"), float(1 << 18), None, ALU.is_lt)
+        tt(R("bb"), R("nd"), R("FF"), ALU.subtract)
+        if t == 0:
+            cp(R("nW"), R("SW", 15, L, 16))
+            ts(R("KK"), R("KA"), 15, None, ALU.bitwise_and)
+            cp(R("BnF"), R("Bn"))
+            ts(R("th"), R("KK"), 1.0, None, ALU.add)
+            tt(R("th"), R("th"), R("bb"), ALU.mult)
+            cp(R("cdU"), R("th"))
+            cp(R("cdR"), X("num", 0, 32, R("cdU")), off=[R("cdU")])
+            ts(R("mk"), R("cdR"), R("pk"), None, ALU.is_equal)
+            tt(R("YY"), R("mk"), R("BnF"), ALU.mult)
+            mm(R("PM", L, 2 * L), R("l16", p=16), R("chh", p=16), True, False)
+            mm(R("PM", L, 2 * L), R("blkf"), R("YY"), False, True)
+        scan(R("SH"), R("rneg"), R("PZ", 0, L), ALU.add, ALU.max)
+        ts(R("srv"), R("PZ", 224, 238), 48.0, None, ALU.is_le)
+        if t == 0:
+            red(R("fc"), R("PZ", 240, 254), ALU.add)
+        cp(R("HI"), R("SH", 15, L, 16))
+        ts(R("HJ"), R("HI"), V - 1, None, ALU.bitwise_and)
+        ts(R("th"), R("bb"), -8192.0, float(NXT), ALU.mult, ALU.add)
+        tt(R("sp"), R("cb"), R("KA"), ALU.subtract)
+        tt(R("th"), R("th"), R("HJ"), ALU.add)
+        tt(R("sp"), R("sp"), R("th"), ALU.max)
+        cp(R("spU"), R("sp"))
+        landed(BIG, NXT, NXT + V, "xr%d" % t, nxt)
+        if t == 0:
+            ts(R("nb"), R("bb"), -1.0, 1.0, ALU.mult, ALU.add)
+            scan(R("SV"), R("rneg"), R("PM", L, 2 * L), ALU.add, ALU.max)
+            tt(R("ta"), R("nb"), R("dW"), ALU.mult)
+            tt(R("th"), R("nb"), R("nW"), ALU.mult)
+            tt(R("oB2"), R("ta"), R("vW0"), ALU.max)
+            tt(R("vW1"), R("SV", 15, L, 16), R("th"), ALU.add)
+            cp(R("oBU"), R("oB2"))
+            cp(R("voff"), R("vW1"))
+        ac(R("NZ"), R("KwT"), AF.Sign)
+        dsub(0, 0)
+        dsub(0, 1)
+        ac(R("SRC"), X(BIG, 0, NXT + V, R("spU")), off=[R("spU")])
+        if t == 0:
+            ac(R("wR"), X("num", 0, V, R("voff")), off=[R("voff")])
+        tt(R("N1"), R("NZ"), R("ramp"), ALU.mult)
+        dsub(0, 2)
+        dA(0, 0)
+        dsub(0, 3)
+        dA(0, 1)
+        mm(R("PZ", 256, 256 + L), R("idn"), R("N1"), True, False)
+        mm(R("PZ", 256, 256 + L), R("idn"), R("KwT"), False, True)
+        tt(R("srv"), R("srv"), R("FF"), ALU.mult)
+        tt(R("srv"), R("srv"), R("bb"), ALU.add)
+        ts(R("ta"), R("srv"), -1.0, 1.0, ALU.mult, ALU.add)
+        tt(R("ta"), R("ta"), R("dW"), ALU.mult)
+        tt(R("oKf"), R("ta"), R(vW), ALU.max)
+        if t == 0:
+            tt(R("Bm"), R("nbrS", 0, 2008, 9), R("JM"), ALU.min)
+            cp(R("oKU", 0, 14), R("oKf"))
+            tt(R("FP"), R("hv"), R("SRC"), ALU.mult)
+            tt(R("Bs"), R("wR"), R("JM"), ALU.subtract)
+            tt(R("Bx"), R("Bm"), R("Bs"), ALU.max)
+            cp(X("nbrS", 0, V + L, R("oBU")), R("Bx"), off=[R("oBU")])
+            tt(X("ringS", 0, V + L, R("oKU", 0, 14)), R("KvT"), R("FP"), ALU.add, off=[R("oKU", 0, 14)])
+            cp(R("BvT"), X("nbrS", 0, V, R("voff")), off=[R("voff")])
+            cp(R("fi"), R("fc"))
+            ts(R("fj"), R("fi"), 15, None, ALU.bitwise_and)
+            tt(R("thr1"), R("fj"), R("thr0"), ALU.add)
+        else:
+            cp(R("oBU"), R("oKf"))
+            cp(R("va"), X("num", 0, V + L, R("oBU")), off=[R("oBU")])
+            cp(R("vWp", 0, 14), R(vW))
+            cp(R("vh"), X("vWp", 0, 14, R("rp")), off=[R("rp")])
+            tt(R("eq"), R("va"), R("vh"), ALU.is_equal)
+            tt(R("eq"), R("eq"), R("tri"), ALU.mult)
+            scan(R("SE"), R("rmul"), R("eq"), ALU.mult, ALU.add)
+            ts(R("ta"), R("SE", 15, L, 16), 0.5, None, ALU.is_ge)
+            tt(R("FP"), R("hv"), R("SRC"), ALU.mult)
+            tt(R("ta"), R("ta"), R("dW"), ALU.mult)
+            tt(R("oKf"), R("oKf"), R("ta"), ALU.max)
+            cp(R("oKU", 0, 28, 2), R("oKf"))
+            for c in range(13, -1, -1):
+                o = R("oKU", 2 * c, 2 * c + 1)
+                tt(X("ringS", 0, V + L, o), R("KvT", 16 * c, 16 * c + 16), R("FP", 16 * c, 16 * c + 16), ALU.add, off=[o])
+            landed("come", 0, 1, "rr", prev)
+            cm = R("come", 0, 1)
+            for m in range(4):
+                a, b = 512 * m, 512 * m + 512
+                ts(R("e1", a, b), R("ringS", a, b), cm, cm, ALU.is_equal, ALU.mult)
+        dA(0, 2)
+        for m in range(4):
+            dsub(1, m)
+            if m == 0:
+                dA(0, 3)
+            dW(0, m)
+            if t == 0 and m == 2:
+                ac(R("V21"), R("wR"), AF.Identity, bias=1.0, scale=2.0)
+        for m in range(4):
+            dA(1, m)
+        for m in range(4):
+            dW(1, m)
+        best(0)
+        ts(R("cap"), R("PA", 0, L), R("thr%d" % t), None, ALU.is_lt)
+        tt(R("com"), R("PZ", 256, 256 + L), R("cap"), ALU.mult)
+        if t == 0:
+            best(1)
+        red(R("rvc"), R("com"), ALU.max)
+        cp(R("rvi"), R("rvc"))
+        ts(R("rvj"), R("rvi"), 255, None, ALU.bitwise_and)
+        if t == 0:
+            cp(R("rv0", 0, 1), R("rvj"))
+            step1(1)
+            remote(T.come[:, 0:1], R("rv0", 0, 1), "rr", "rl", nxt)
+            revoke(0, R("rv0", 0, 1), "ringS", ("PC0", "PC1", "PK", "PD0"))
+            remote(T.BIG1[:, NXT:NXT + V], R("ringS", 0, V), "xr1", "xl1", prev)
+            ac(R("KvT"), X("ringS", 0, V, R("voff")), off=[R("voff")])
+        else:
+            cp(R("rv1", 0, 1), R("rvj"))
+            tt(R("tmpc"), R("rv1", 0, 1), cm, ALU.not_equal)
+            tt(R("rv1", 1, 2), R("rv1", 0, 1), R("tmpc"), ALU.mult)
+            revoke(1, R("rv1", 1, 2), "ykS", ("PC0", "PC1", "PK", "PA"))
+            best(1)
+            dma("Y", T.yz[:, :], T.zf[:, :], rd=[R("zf")])
+    for s, c in total.items():
+        if known["Y"].get(s, 0) < c:
+            g.sync.wait_ge(T.sem[s], c)

@@ -4,7 +4,8 @@ L, V = 224, 2048
 CH = [(0, 128), (128, 224)]
 BASE = [0, 17 * 128]
 NXT = 17 * 224
-SCRATCH, SMALL = {}, {}
+SCRATCH, SMALL, PLAN = {}, {}, []
+SPLIT = ("M2", "MM", "PR", "PI", "PJ", "ZS", "ZI")
 for _n, _w, _d in (
         ("ringS", V + L, "bfloat16"), ("nbrS", V + L, "int32"), ("matS", 4096, "bfloat16"), ("thrI", 1, "int32"),
         ("num", V + L, "float32"), ("BIG0", NXT + V, "bfloat16"), ("BIG1", NXT + V, "bfloat16"),
@@ -21,11 +22,11 @@ for _n, _w, _d in (
         ("JI", L, "int32"), ("JM", L, "int32"), ("YY", L, "float32"), ("SW", L, "float32"), ("nW", 14, "float32"),
         ("noff", 14, "uint16"), ("Bn", L, "uint16"), ("BnF", L, "float32"), ("BvT", L, "int32"), ("KvT", L, "bfloat16"),
         ("hv", L, "bfloat16"), ("hn", L, "bfloat16"), ("E3", L, "bfloat16"),
-        ("M2", 128, "float32"), ("MM", 128, "float32"), ("SK", L, "float32"), ("SD", L, "float32"),
+        ("M2", L, "float32"), ("MM", L, "float32"), ("SK", L, "float32"), ("SD", L, "float32"),
         ("posU", 14, "uint16"), ("KI", 14, "int32"), ("KA", 14, "int32"), ("KK", 14, "int32"), ("xn", 14, "float32"),
-        ("bb", 14, "float32"), ("nb", 14, "float32"), ("nd", 14, "float32"), ("PR", 128, "float32"), ("PI", 128, "int32"),
-        ("PJ", 128, "int32"), ("PL", L, "uint16"), ("KwT", L, "bfloat16"), ("DI", 14, "int32"), ("DA", 14, "int32"),
-        ("pxU", 14, "uint16"), ("ZS", 128, "float32"), ("ZI", 128, "int32"),
+        ("bb", 14, "float32"), ("nb", 14, "float32"), ("nd", 14, "float32"), ("PR", L, "float32"), ("PI", L, "int32"),
+        ("PJ", L, "int32"), ("ths", 14, "float32"), ("thn", 14, "float32"), ("taB", 14, "float32"), ("taD", 14, "float32"), ("YW", L, "float32"), ("PL", L, "uint16"), ("KwT", L, "bfloat16"), ("DI", 14, "int32"), ("DA", 14, "int32"),
+        ("pxU", 14, "uint16"), ("ZS", L, "float32"), ("ZI", L, "int32"),
         ("NZ", L, "bfloat16"), ("N1", L, "bfloat16"), ("cap", L, "float32"), ("com", L, "float32"), ("rvc", 1, "float32"),
         ("rvi", 1, "int32"), ("rvj", 1, "int32"), ("rv0", 4, "float32"), ("rv1", 4, "float32"), ("come", 4, "float32"), ("HZ", L, "float32"),
         ("SH", L, "float32"), ("HI", 14, "int32"), ("HJ", 14, "int32"), ("FF", 14, "bfloat16"), ("Finc", 14, "bfloat16"),
@@ -104,19 +105,86 @@ def rank_program(g, core, T, topo):
                 known[e][a] = max(known[e].get(a, 0), b)
             known[e][s] = max(known[e].get(s, 0), c)
 
-    def emit(e, fn, reads, writes, sem=None, inc=1):
-        s = sem or semof[e]
-        rd = [r[1:] for r in reads]
-        wr = [r[1:] for r in writes]
-        waits(e, need(e, rd, False) + need(e, wr, True))
-        fn().then_inc(T.sem[s], inc)
+    ops = []
+
+    def emit(e, fn, reads, writes, sem=None, inc=1, cost=0.06, lat=0.1):
+        ops.append((e, fn, [r[1:] for r in reads], [r[1:] for r in writes], sem or semof[e], inc, cost, lat))
+
+    def issue(e, fn, rd, wr, s, inc, cost, lat):
+        if e != "R":
+            waits(e, need(e, rd, False) + need(e, wr, True))
+            ins = fn()
+            if ins is not None:
+                ins.then_inc(T.sem[s], inc)
         total[s] = total.get(s, 0) + inc
-        snap = dict(known[e])
+        snap = dict(known[e]) if e != "R" else {}
         snap[s] = total[s]
         note(e, rd, False, s, total[s], snap)
         note(e, wr, True, s, total[s], snap)
 
+    def order():
+        succ, npred, acc = [[] for _ in ops], [0] * len(ops), {}
+        for i, (e, fn, rd, wr, s, inc, cost, lat) in enumerate(ops):
+            before = {}
+            for refs, write in ((rd, False), (wr, True)):
+                for name, lo, hi, tag in refs:
+                    for (l2, h2, w2, j, t2) in acc.get(name, ()):
+                        same = ops[j][0] == e
+                        if name in BANKS:
+                            if same and not (write and w2):
+                                continue
+                            d = 0.0 if same else ops[j][7]
+                        else:
+                            if not (l2 < hi and lo < h2) or not (write or w2) or (tag and t2 and tag[0] == t2[0] and tag[1] != t2[1]):
+                                continue
+                            d = 0.0 if same and not w2 else ops[j][7]
+                        before[j] = max(before.get(j, 0.0), d)
+            for refs, write in ((rd, False), (wr, True)):
+                for name, lo, hi, tag in refs:
+                    a = acc.setdefault(name, [])
+                    if write and name in BANKS:
+                        a[:] = [x for x in a if ops[x[3]][0] == e and not x[2]]
+                    elif write:
+                        a[:] = [x for x in a if not (lo <= x[0] and x[1] <= hi and tag in (None, x[4]))]
+                    a.append((lo, hi, write, i, tag))
+            for j, d in before.items():
+                if j != i:
+                    succ[j].append((i, d))
+                    npred[i] += 1
+        rank_ = [0.0] * len(ops)
+        for i in range(len(ops) - 1, -1, -1):
+            rank_[i] = ops[i][6] + max([d + rank_[k] for k, d in succ[i]] + [0.0])
+        ready = {e: [] for e in ("V", "S", "P", "G", "Y", "R")}
+        rt, free, out = [0.0] * len(ops), {e: 0.0 for e in ready}, []
+        for i, n in enumerate(npred):
+            if n == 0:
+                ready[ops[i][0]].append(i)
+        while len(out) < len(ops):
+            start, e = min((max(free[e], min(rt[i] for i in ready[e])), e) for e in ready if ready[e])
+            i = min(ready[e]) if e == "Y" else max((k for k in ready[e] if rt[k] <= start + 0.01), key=lambda k: (rank_[k], -k))
+            ready[e].remove(i)
+            out.append(i)
+            end = max(start, rt[i]) + ops[i][6]
+            free[e] = end
+            for k, d in succ[i]:
+                rt[k] = max(rt[k], end + d)
+                npred[k] -= 1
+                if npred[k] == 0:
+                    ready[ops[k][0]].append(k)
+        return out
+
+    def width(r):
+        return r[3] - r[2] if r[4] is None or r[4][0] in ("k", "q") else (r[3] - r[2] + r[4][0] - 1) // r[4][0]
+
+    def wide(*refs):
+        return all(SCRATCH[r[1]][0] == "sbuf" and SCRATCH[r[1]][2] in ("bfloat16", "uint16") for r in refs)
+
+    def vcost(n, per):
+        return 0.00083 * max(64, n * per)
+
     def R(name, lo=0, hi=None, step=1, p=None):
+        if name in SPLIT and lo == 0 and hi == 96:
+            lo, hi = 128, 224
         if name in SMALL:
             name, off, w = SMALL[name]
             lo, hi = lo + off, off + (w if hi is None else hi)
@@ -140,66 +208,73 @@ def rank_program(g, core, T, topo):
 
     def ts(out, a, s1, s2, op0, op1=None):
         rd = [a] + cols(s1, s2)
+        c = vcost(width(out), 0.5 if wide(out, a) else 1)
         if op1 is None:
-            emit("V", lambda: g.vector.tensor_scalar(out[0], a[0], val(s1), None, op0), rd, [out])
+            emit("V", lambda: g.vector.tensor_scalar(out[0], a[0], val(s1), None, op0), rd, [out], cost=c)
         else:
-            emit("V", lambda: g.vector.tensor_scalar(out[0], a[0], val(s1), val(s2), op0, op1), rd, [out])
+            emit("V", lambda: g.vector.tensor_scalar(out[0], a[0], val(s1), val(s2), op0, op1), rd, [out], cost=c)
 
     def tt(out, a, b, op, off=()):
-        emit("V", lambda: g.vector.tensor_tensor(out[0], a[0], b[0], op), [a, b] + list(off), [out])
+        n = width(b)
+        c = vcost(n, 1 if a[1] in BANKS or b[1] in BANKS else 2)
+        if off:
+            c = 0.05 + vcost(n, 1.6 if a[3] - a[2] > n else 3.8)
+        emit("V", lambda: g.vector.tensor_tensor(out[0], a[0], b[0], op), [a, b] + list(off), [out], cost=c)
 
     def cp(out, a, off=()):
-        emit("V", lambda: g.vector.tensor_copy(out[0], a[0]), [a] + list(off), [out])
+        n = min(width(out), width(a))
+        c = 0.05 + vcost(n, 1.6 if width(out) <= width(a) else 3.8) if off else vcost(n, 0.5 if wide(out, a) else 1)
+        emit("V", lambda: g.vector.tensor_copy(out[0], a[0]), [a] + list(off), [out], cost=c)
 
     def scan(out, d0, d1, op0, op1):
-        emit("V", lambda: g.vector.tensor_tensor_scan(out[0], d0[0], d1[0], 0.0, op0, op1), [d0, d1], [out])
+        emit("V", lambda: g.vector.tensor_tensor_scan(out[0], d0[0], d1[0], 0.0, op0, op1), [d0, d1], [out], cost=vcost(width(out), 1))
 
     def red(out, a, op):
-        emit("V", lambda: g.vector.tensor_reduce(out[0], a[0], AxisListType.X, op), [a], [out])
+        emit("V", lambda: g.vector.tensor_reduce(out[0], a[0], AxisListType.X, op), [a], [out], cost=vcost(width(a), 1))
 
     def ac(out, a, func=AF.Copy, off=(), **kw):
-        emit("S", lambda: g.scalar.activation(out[0], a[0], func, **kw), [a] + list(off), [out])
+        n = width(out)
+        emit("S", lambda: g.scalar.activation(out[0], a[0], func, **kw), [a] + list(off), [out], cost=0.065 + vcost(n, 1.6) if off else vcost(n, 1))
 
     def fill(out, c):
-        emit("V", lambda: g.vector.memset(out[0], c), [], [out])
+        emit("V", lambda: g.vector.memset(out[0], c), [], [out], cost=vcost(width(out), 1))
 
     def mm(out, lhsT, rhs, start, stop):
-        emit("P", lambda: g.tensor.matmul(out[0], lhsT[0], rhs[0], start, stop), [lhsT, rhs], [out])
+        c = 0.00042 * max(64, width(out)) * (1 if wide(rhs) else 4)
+        emit("P", lambda: g.tensor.matmul(out[0], lhsT[0], rhs[0], start, stop), [lhsT, rhs], [out], cost=c)
 
     def iota(out, pattern, base, cm):
-        emit("G", lambda: g.iota(out[0], pattern, base, cm, allow_small_or_imprecise_dtypes=True), [], [out])
+        c = 0.13 + vcost(width(out), 2)
+        emit("G", lambda: g.iota(out[0], pattern, base, cm, allow_small_or_imprecise_dtypes=True), [], [out], cost=c)
 
     def asel(out, a, pattern, op, fillv, base, cm):
-        emit("G", lambda: g.affine_select(out[0], a[0], pattern, op, fillv, base, cm), [a], [out])
+        c = 0.17 + vcost(width(out), 2)
+        emit("G", lambda: g.affine_select(out[0], a[0], pattern, op, fillv, base, cm), [a], [out], cost=c)
 
     ndma = [0]
 
     def dma(e, out, a, rd=(), wr=()):
         s = "d%d" % ndma[0]
         ndma[0] += 1
-        emit(e, lambda: queue[e].dma_start(out, a), list(rd), list(wr), s, 16)
+        n = sum(width(r) for r in wr)
+        emit(e, lambda: queue[e].dma_start(out, a), list(rd), list(wr), s, 16, lat=2.0 + n * 0.002)
 
     def remote(out_ap, src, rsem, lsem, dst):
         rid, pid, _ = topo.addr(dst)
-        n = len(topo.engines(core, dst))
-        waits("G", need("G", [src[1:]], False))
-        g.remote_dma(out_ap, src[0], T.sem[rsem], T.sem[lsem], pid, rid, topo.mask(core, dst))
-        total[lsem] = total.get(lsem, 0) + n
-        snap = dict(known["G"])
-        snap[lsem] = total[lsem]
-        note("G", [src[1:]], False, lsem, total[lsem], snap)
 
-    def landed(name, lo, hi, rsem, src):
-        n = len(topo.engines(src, core))
-        total[rsem] = total.get(rsem, 0) + n
-        note("R", [(name, lo, hi, None)], True, rsem, total[rsem], {rsem: total[rsem]})
+        def call():
+            g.remote_dma(out_ap, src[0], T.sem[rsem], T.sem[lsem], pid, rid, topo.mask(core, dst))
+        emit("G", call, [src], [(None, lsem, 0, 1, None)], lsem, len(topo.engines(core, dst)), 1.0, 9.0)
+
+    def landed(name, lo, hi, rsem, lsem, src):
+        emit("R", None, [(None, lsem, 0, 1, None)], [(None, name, lo, hi, None)], rsem, len(topo.engines(src, core)), 0.0, 0.0)
 
     prev, nxt = T.cores[(rank - 1) % N], T.cores[(rank + 1) % N]
     dma("Y", T.zb0[:, :], T.z0[:, :], wr=[R("zb0")])
     dma("Y", T.nbrS[:, 0:V], T.nbr[:, :], wr=[R("nbrS", 0, V)])
-    dma("S", T.ringS[:, 0:V], T.ring[:, :], wr=[R("ringS", 0, V)])
-    dma("S", T.thrI[:, :], T.thr[:, :], wr=[R("thrI")])
+    dma("Y", T.ringS[:, 0:V], T.ring[:, :], wr=[R("ringS", 0, V)])
     dma("Y", T.matS[:, :], T.mat[:, :], wr=[R("matS")])
+    dma("Y", T.thrI[:, :], T.thr[:, :], wr=[R("thrI")])
     fill(R("ones"), 1.0)
     fill(R("sel1"), 0.0)
     fill(R("sel1", 15, 143, 16), 1.0)
@@ -435,28 +510,28 @@ def rank_program(g, core, T, topo):
             cp(R("cdU"), R("th"))
             cp(R("cdR"), X("num", 0, 32, R("cdU")), off=[R("cdU")])
             ts(R("mk"), R("cdR"), R("pk"), None, ALU.is_equal)
-            tt(R("YY"), R("mk"), R("BnF"), ALU.mult)
+            tt(R("YW"), R("mk"), R("BnF"), ALU.mult)
             mm(R("PM", L, 2 * L), R("l16", p=16), R("chh", p=16), True, False)
-            mm(R("PM", L, 2 * L), R("blkf"), R("YY"), False, True)
+            mm(R("PM", L, 2 * L), R("blkf"), R("YW"), False, True)
         scan(R("SH"), R("rneg"), R("PZ", 0, L), ALU.add, ALU.max)
         ts(R("srv"), R("PZ", 224, 238), 48.0, None, ALU.is_le)
         if t == 0:
             red(R("fc"), R("PZ", 240, 254), ALU.add)
         cp(R("HI"), R("SH", 15, L, 16))
         ts(R("HJ"), R("HI"), V - 1, None, ALU.bitwise_and)
-        ts(R("th"), R("bb"), -8192.0, float(NXT), ALU.mult, ALU.add)
+        ts(R("ths"), R("bb"), -8192.0, float(NXT), ALU.mult, ALU.add)
         tt(R("sp"), R("cb"), R("KA"), ALU.subtract)
-        tt(R("th"), R("th"), R("HJ"), ALU.add)
-        tt(R("sp"), R("sp"), R("th"), ALU.max)
+        tt(R("ths"), R("ths"), R("HJ"), ALU.add)
+        tt(R("sp"), R("sp"), R("ths"), ALU.max)
         cp(R("spU"), R("sp"))
-        landed(BIG, NXT, NXT + V, "xr%d" % t, nxt)
+        landed(BIG, NXT, NXT + V, "xr%d" % t, "xl%d" % t, nxt)
         if t == 0:
             ts(R("nb"), R("bb"), -1.0, 1.0, ALU.mult, ALU.add)
             scan(R("SV"), R("rneg"), R("PM", L, 2 * L), ALU.add, ALU.max)
-            tt(R("ta"), R("nb"), R("dW"), ALU.mult)
-            tt(R("th"), R("nb"), R("nW"), ALU.mult)
-            tt(R("oB2"), R("ta"), R("vW0"), ALU.max)
-            tt(R("vW1"), R("SV", 15, L, 16), R("th"), ALU.add)
+            tt(R("taB"), R("nb"), R("dW"), ALU.mult)
+            tt(R("thn"), R("nb"), R("nW"), ALU.mult)
+            tt(R("oB2"), R("taB"), R("vW0"), ALU.max)
+            tt(R("vW1"), R("SV", 15, L, 16), R("thn"), ALU.add)
             cp(R("oBU"), R("oB2"))
             cp(R("voff"), R("vW1"))
         ac(R("NZ"), R("KwT"), AF.Sign)
@@ -505,7 +580,7 @@ def rank_program(g, core, T, topo):
             for c in range(13, -1, -1):
                 o = R("oKU", 2 * c, 2 * c + 1)
                 tt(X("ringS", 0, V + L, o), R("KvT", 16 * c, 16 * c + 16), R("FP", 16 * c, 16 * c + 16), ALU.add, off=[o])
-            landed("come", 0, 1, "rr", prev)
+            landed("come", 0, 1, "rr", "rl", prev)
             cm = R("come", 0, 1)
             for m in range(4):
                 a, b = 512 * m, 512 * m + 512
@@ -544,6 +619,10 @@ def rank_program(g, core, T, topo):
             revoke(1, R("rv1", 1, 2), "ykS", ("PC0", "PC1", "PK", "PA"))
             best(1)
             dma("Y", T.yz[:, :], T.zf[:, :], rd=[R("zf")])
+    if not PLAN:
+        PLAN.extend(order())
+    for i in PLAN:
+        issue(*ops[i])
     for s, c in total.items():
         if known["Y"].get(s, 0) < c:
             g.sync.wait_ge(T.sem[s], c)

from concourse.mybir import AluOpType as ALU, AxisListType, ActivationFunctionType as AF

L, V = 224, 2048
CH = [(0, 128), (128, 224)]
BASE = [0, 17 * 128]
NXT = 17 * 224
SCRATCH, SMALL, PLAN = {}, {}, []
SPLIT = ("M2", "MM", "PR", "PI", "PJ", "ZS", "ZI")
for _n, _w, _d in (
        ("ringS", V + L, "bfloat16"), ("nbrS", V + L, "int32"), ("matS", 4096, "bfloat16"), ("thrI", 1, "int32"),
        ("num", V + L, "float32"), ("BIG0", NXT + V, "bfloat16"), ("BIG1", NXT + V, "bfloat16"),
        ("zb0", L, "bfloat16"), ("zb1", L, "bfloat16"), ("zf", L, "float32"), ("XC0", 2048, "bfloat16"), ("XC1", 1536, "bfloat16"),
        ("ones", 256, "bfloat16"), ("sel1", 144, "bfloat16"), ("selk", 144, "bfloat16"), ("selm", 144, "bfloat16"),
        ("blk", 128, "bfloat16"), ("blkz", 128, "bfloat16"), ("blkf", 128, "float32"), ("trid", 128, "bfloat16"),
        ("idn", 128, "bfloat16"), ("nidn", 128, "bfloat16"), ("l16", 128, "bfloat16"), ("cn", L, "bfloat16"), ("chh", L, "bfloat16"),
        ("rowA", 128, "bfloat16"), ("rowB", 128, "bfloat16"), ("rneg", L, "float32"), ("rmul", L, "float32"), ("ramp", L, "bfloat16"),
        ("tri", L, "bfloat16"), ("zer", 16, "float32"), ("pI", 1, "int32"), ("qI", 1, "int32"), ("qc", 1, "float32"),
        ("pc0", 1, "float32"), ("pc1", 1, "float32"), ("tp0", 1, "float32"), ("tp1", 1, "float32"), ("pk", 1, "float32"),
        ("thr0", 1, "float32"), ("thr1", 1, "float32"), ("tmpc", 1, "float32"), ("rowc", 16, "float32"),
        ("iW", 14, "float32"), ("nk", 14, "float32"), ("dW", 14, "float32"), ("cb", 14, "float32"), ("vW0", 14, "float32"),
        ("vW1", 14, "float32"), ("V20", L, "float32"), ("V21", L, "float32"),
        ("JI", L, "int32"), ("JM", L, "int32"), ("YY", L, "float32"), ("SW", L, "float32"), ("nW", 14, "float32"),
        ("noff", 14, "uint16"), ("Bn", L, "uint16"), ("BnF", L, "float32"), ("BvT", L, "int32"), ("KvT", L, "bfloat16"),
        ("hv", L, "bfloat16"), ("hn", L, "bfloat16"), ("E3", L, "bfloat16"),
        ("M2", L, "float32"), ("MM", L, "float32"), ("SK", L, "float32"), ("SD", L, "float32"),
        ("posU", 14, "uint16"), ("KI", 14, "int32"), ("KA", 14, "int32"), ("KK", 14, "int32"), ("xn", 14, "float32"),
        ("bb", 14, "float32"), ("nb", 14, "float32"), ("nd", 14, "float32"), ("PR", L, "float32"), ("PI", L, "int32"),
        ("PJ", L, "int32"), ("ths", 14, "float32"), ("thn", 14, "float32"), ("taB", 14, "float32"), ("taD", 14, "float32"), ("YW", L, "float32"), ("PL", L, "uint16"), ("KwT", L, "bfloat16"), ("DI", 14, "int32"), ("DA", 14, "int32"),
        ("pxU", 14, "uint16"), ("ZS", L, "float32"), ("ZI", L, "int32"),
        ("NZ", L, "bfloat16"), ("N1", L, "bfloat16"), ("cap", L, "float32"), ("com", L, "float32"), ("rvc", 1, "float32"),
        ("rvi", 1, "int32"), ("rvj", 1, "int32"), ("rv0", 4, "float32"), ("rv1", 4, "float32"), ("come", 4, "float32"), ("HZ", L, "float32"),
        ("SH", L, "float32"), ("HI", 14, "int32"), ("HJ", 14, "int32"), ("FF", 14, "bfloat16"), ("Finc", 14, "bfloat16"),
        ("srv", 14, "float32"), ("th", 14, "float32"), ("sp", 14, "float32"), ("spU", 14, "uint16"),
        ("SRC", L, "bfloat16"), ("FP", L, "bfloat16"), ("ta", 14, "float32"), ("oKf", 14, "float32"), ("oKU", 28, "uint16"),
        ("oBU", 14, "uint16"), ("oB2", 14, "float32"), ("cdU", 14, "uint16"), ("cdR", L, "float32"), ("mk", L, "float32"), ("SV", L, "float32"),
        ("voff", 14, "uint16"), ("wR", L, "float32"), ("Bm", L, "float32"), ("Bs", L, "float32"), ("Bx", L, "int32"),
        ("fc", 1, "float32"), ("fi", 1, "int32"), ("fj", 1, "int32"),
        ("rpI", L, "int32"), ("rp", 14, "uint16"), ("vh", L, "float32"), ("va", L, "float32"), ("eq", L, "float32"), ("SE", L, "float32"),
        ("e0", V, "bfloat16"), ("e1", V, "bfloat16"), ("ykS", V, "bfloat16"), ("vWp", 16, "float32")):
    if _w in (1, 14) and _d != "uint16" and _n not in ("thrI", "FF", "Finc"):
        _b = "small" + _d
        SMALL[_n] = (_b, 16 * len(SMALL), _w)
        SCRATCH[_b] = ("sbuf", [128, 16 * len(SMALL)], _d)
    else:
        SCRATCH[_n] = ("sbuf", [128, _w], _d)
for _n in ("E1", "E2", "DD"):
    SCRATCH[_n] = ("sbuf", [128, L, 16], "bfloat16")
BANKS = ("PZ", "PK", "PC0", "PC1", "PD0", "PD1", "PA", "PM")
for _n in BANKS:
    SCRATCH[_n] = ("psum", [128, 512], "float32")
SEMAPHORES = ["sV", "sS", "sP", "sG", "xr0", "xr1", "xl0", "xl1", "rr", "rl"] + ["d%d" % i for i in range(16)]


def rank_program(g, core, T, topo):
    rank = T.rank_of(core)
    if rank is None:
        return
    N = len(T.cores)
    queue = {"V": g.vector, "S": g.scalar, "P": g.tensor, "G": g, "Y": g.sync}
    semof = {"V": "sV", "S": "sS", "P": "sP", "G": "sG"}
    total = {}
    known = {e: {} for e in queue}
    log = {}

    def need(e, refs, write):
        out = []
        for name, lo, hi, tag in refs:
            for (l2, h2, w2, e2, s2, c2, k2, t2) in log.get(name, ()):
                if name in BANKS:
                    if e2 == e and (write or not w2):
                        continue
                else:
                    if not (l2 < hi and lo < h2) or not (write or w2):
                        continue
                    if tag and t2 and tag[0] == t2[0] and tag[1] != t2[1]:
                        continue
                    if e2 == e and s2 == semof.get(e) and not w2:
                        continue
                out.append((s2, c2, k2))
        return out

    def note(e, refs, write, s, c, snap):
        for name, lo, hi, tag in refs:
            acc = log.setdefault(name, [])
            if name in BANKS:
                acc[:] = [a for a in acc if not (a[3] == e and a[2] == write)]
            elif write:
                acc[:] = [a for a in acc if not (lo <= a[0] and a[1] <= hi and tag in (None, a[7]))]
            else:
                acc[:] = [a for a in acc if a[2] or not (a[3] == e and a[4] == s and lo <= a[0] and a[1] <= hi and tag in (None, a[7]))]
            acc.append((lo, hi, write, e, s, c, snap, tag))

    def waits(e, deps):
        todo = {}
        for s, c, k in deps:
            if known[e].get(s, 0) < c and todo.get(s, (0,))[0] < c:
                todo[s] = (c, k)
        for s in list(todo):
            c = todo[s][0]
            if any(o != s and todo[o][1].get(s, 0) >= c for o in todo):
                del todo[s]
        for s, (c, k) in todo.items():
            queue[e].wait_ge(T.sem[s], c)
            for a, b in k.items():
                known[e][a] = max(known[e].get(a, 0), b)
            known[e][s] = max(known[e].get(s, 0), c)

    ops = []

    def emit(e, fn, reads, writes, sem=None, inc=1, cost=0.06, lat=0.1):
        ops.append((e, fn, [r[1:] for r in reads], [r[1:] for r in writes], sem or semof[e], inc, cost, lat))

    def issue(e, fn, rd, wr, s, inc, cost, lat):
        if e != "R":
            waits(e, need(e, rd, False) + need(e, wr, True))
            ins = fn()
            if ins is not None:
                ins.then_inc(T.sem[s], inc)
        total[s] = total.get(s, 0) + inc
        snap = dict(known[e]) if e != "R" else {}
        snap[s] = total[s]
        note(e, rd, False, s, total[s], snap)
        note(e, wr, True, s, total[s], snap)

    def order():
        succ, npred, acc = [[] for _ in ops], [0] * len(ops), {}
        for i, (e, fn, rd, wr, s, inc, cost, lat) in enumerate(ops):
            before = {}
            for refs, write in ((rd, False), (wr, True)):
                for name, lo, hi, tag in refs:
                    for (l2, h2, w2, j, t2) in acc.get(name, ()):
                        same = ops[j][0] == e
                        if name in BANKS:
                            if same and not (write and w2):
                                continue
                            d = 0.0 if same else ops[j][7]
                        else:
                            if not (l2 < hi and lo < h2) or not (write or w2) or (tag and t2 and tag[0] == t2[0] and tag[1] != t2[1]):
                                continue
                            d = 0.0 if same and not w2 else ops[j][7]
                        before[j] = max(before.get(j, 0.0), d)
            for refs, write in ((rd, False), (wr, True)):
                for name, lo, hi, tag in refs:
                    a = acc.setdefault(name, [])
                    if write and name in BANKS:
                        a[:] = [x for x in a if ops[x[3]][0] == e and not x[2]]
                    elif write:
                        a[:] = [x for x in a if not (lo <= x[0] and x[1] <= hi and tag in (None, x[4]))]
                    a.append((lo, hi, write, i, tag))
            for j, d in before.items():
                if j != i:
                    succ[j].append((i, d))
                    npred[i] += 1
        rank_ = [0.0] * len(ops)
        for i in range(len(ops) - 1, -1, -1):
            rank_[i] = ops[i][6] + max([d + rank_[k] for k, d in succ[i]] + [0.0])
        ready = {e: [] for e in ("V", "S", "P", "G", "Y", "R")}
        rt, free, out = [0.0] * len(ops), {e: 0.0 for e in ready}, []
        for i, n in enumerate(npred):
            if n == 0:
                ready[ops[i][0]].append(i)
        while len(out) < len(ops):
            start, e = min((max(free[e], min(rt[i] for i in ready[e])), e) for e in ready if ready[e])
            i = min(ready[e]) if e == "Y" else max((k for k in ready[e] if rt[k] <= start + 0.01), key=lambda k: (rank_[k], -k))
            ready[e].remove(i)
            out.append(i)
            end = max(start, rt[i]) + ops[i][6]
            free[e] = end
            for k, d in succ[i]:
                rt[k] = max(rt[k], end + d)
                npred[k] -= 1
                if npred[k] == 0:
                    ready[ops[k][0]].append(k)
        return out

    def width(r):
        return r[3] - r[2] if r[4] is None or r[4][0] in ("k", "q") else (r[3] - r[2] + r[4][0] - 1) // r[4][0]

    def wide(*refs):
        return all(SCRATCH[r[1]][0] == "sbuf" and SCRATCH[r[1]][2] in ("bfloat16", "uint16") for r in refs)

    def vcost(n, per):
        return 0.00083 * max(64, n * per)

    def R(name, lo=0, hi=None, step=1, p=None):
        if name in SPLIT and lo == 0 and hi == 96:
            lo, hi = 128, 224
        if name in SMALL:
            name, off, w = SMALL[name]
            lo, hi = lo + off, off + (w if hi is None else hi)
        hi = T[name].shape[1] if hi is None else hi
        ps = slice(None) if p is None else slice(0, p)
        ap = T[name][ps, lo:hi] if step == 1 else T[name][ps, lo:hi:step]
        return (ap, name, lo, hi, None if step == 1 else (step, lo % step))

    def X(name, lo, hi, off):
        return (T[name][:, lo:hi].indirect(off[0]), name, lo, hi, None)

    def E3d(name, l0, l1, k=None, q=None):
        ap = T[name][:, l0:l1, k] if k is not None else T[name][:, l0 + q:l1:16, :]
        return (ap, name, l0, l1, ("q", q) if k is None else ("k", k))

    def cols(*xs):
        return [x for x in xs if isinstance(x, tuple)]

    def val(x):
        return x[0] if isinstance(x, tuple) else x

    def ts(out, a, s1, s2, op0, op1=None):
        rd = [a] + cols(s1, s2)
        c = vcost(width(out), 0.5 if wide(out, a) else 1)
        if op1 is None:
            emit("V", lambda: g.vector.tensor_scalar(out[0], a[0], val(s1), None, op0), rd, [out], cost=c)
        else:
            emit("V", lambda: g.vector.tensor_scalar(out[0], a[0], val(s1), val(s2), op0, op1), rd, [out], cost=c)

    def tt(out, a, b, op, off=()):
        n = width(b)
        c = vcost(n, 1 if a[1] in BANKS or b[1] in BANKS else 2)
        if off:
            c = 0.05 + vcost(n, 1.6 if a[3] - a[2] > n else 3.8)
        emit("V", lambda: g.vector.tensor_tensor(out[0], a[0], b[0], op), [a, b] + list(off), [out], cost=c)

    def cp(out, a, off=()):
        n = min(width(out), width(a))
        c = 0.05 + vcost(n, 1.6 if width(out) <= width(a) else 3.8) if off else vcost(n, 0.5 if wide(out, a) else 1)
        emit("V", lambda: g.vector.tensor_copy(out[0], a[0]), [a] + list(off), [out], cost=c)

    def scan(out, d0, d1, op0, op1):
        emit("V", lambda: g.vector.tensor_tensor_scan(out[0], d0[0], d1[0], 0.0, op0, op1), [d0, d1], [out], cost=vcost(width(out), 1))

    def red(out, a, op):
        emit("V", lambda: g.vector.tensor_reduce(out[0], a[0], AxisListType.X, op), [a], [out], cost=vcost(width(a), 1))

    def ac(out, a, func=AF.Copy, off=(), **kw):
        n = width(out)
        emit("S", lambda: g.scalar.activation(out[0], a[0], func, **kw), [a] + list(off), [out], cost=0.065 + vcost(n, 1.6) if off else vcost(n, 1))

    def fill(out, c):
        emit("V", lambda: g.vector.memset(out[0], c), [], [out], cost=vcost(width(out), 1))

    def mm(out, lhsT, rhs, start, stop):
        c = 0.00042 * max(64, width(out)) * (1 if wide(rhs) else 4)
        emit("P", lambda: g.tensor.matmul(out[0], lhsT[0], rhs[0], start, stop), [lhsT, rhs], [out], cost=c)

    def iota(out, pattern, base, cm):
        c = 0.13 + vcost(width(out), 2)
        emit("G", lambda: g.iota(out[0], pattern, base, cm, allow_small_or_imprecise_dtypes=True), [], [out], cost=c)

    def asel(out, a, pattern, op, fillv, base, cm):
        c = 0.17 + vcost(width(out), 2)
        emit("G", lambda: g.affine_select(out[0], a[0], pattern, op, fillv, base, cm), [a], [out], cost=c)

    ndma = [0]

    def dma(e, out, a, rd=(), wr=()):
        s = "d%d" % ndma[0]
        ndma[0] += 1
        n = sum(width(r) for r in wr)
        emit(e, lambda: queue[e].dma_start(out, a), list(rd), list(wr), s, 16, lat=2.0 + n * 0.002)

    def remote(out_ap, src, rsem, lsem, dst):
        rid, pid, _ = topo.addr(dst)

        def call():
            g.remote_dma(out_ap, src[0], T.sem[rsem], T.sem[lsem], pid, rid, topo.mask(core, dst))
        emit("G", call, [src], [(None, lsem, 0, 1, None)], lsem, len(topo.engines(core, dst)), 1.0, 9.0)

    def landed(name, lo, hi, rsem, lsem, src):
        emit("R", None, [(None, lsem, 0, 1, None)], [(None, name, lo, hi, None)], rsem, len(topo.engines(src, core)), 0.0, 0.0)

    prev, nxt = T.cores[(rank - 1) % N], T.cores[(rank + 1) % N]
    dma("Y", T.zb0[:, :], T.z0[:, :], wr=[R("zb0")])
    dma("Y", T.nbrS[:, 0:V], T.nbr[:, :], wr=[R("nbrS", 0, V)])
    dma("Y", T.ringS[:, 0:V], T.ring[:, :], wr=[R("ringS", 0, V)])
    dma("Y", T.matS[:, :], T.mat[:, :], wr=[R("matS")])
    dma("Y", T.thrI[:, :], T.thr[:, :], wr=[R("thrI")])
    fill(R("ones"), 1.0)
    fill(R("sel1"), 0.0)
    fill(R("sel1", 15, 143, 16), 1.0)
    iota(R("pI"), [[1, 1]], 0, 1)
    o8 = R("ones", 0, 128)
    asel(R("blk"), o8, [[-16, 8], [0, 16]], ALU.is_ge, 0.0, 0, 1)
    asel(R("blk"), R("blk"), [[16, 8], [0, 16]], ALU.is_ge, 0.0, 15, -1)
    asel(R("idn"), o8, [[-1, 128]], ALU.is_equal, 0.0, 0, 1)
    asel(R("l16", p=16), R("ones", 0, 128, p=16), [[0, 8], [-1, 16]], ALU.is_equal, 0.0, 0, 1)
    asel(R("cn", p=16), R("ones", 0, L, p=16), [[0, 14], [-1, 16]], ALU.is_equal, 0.0, 0, 1)
    s8 = R("sel1", 15, 143, 16)
    asel(s8, s8, [[-16, 8]], ALU.is_ge, 0.0, 0, 1)
    asel(s8, s8, [[16, 8]], ALU.is_ge, 0.0, 15, -1)
    iota(R("rowA"), [[-256, 8], [0, 16]], 1792, 0)
    iota(R("rowB"), [[0, 8], [-1, 16]], 255, -16)
    iota(R("rowc", 0, 14), [[16, 14]], 0, 0)
    iota(R("V20"), [[18, L]], 1, 0)
    iota(R("ramp"), [[-256, L]], 256 * L, 0)
    asel(R("trid"), R("blk"), [[-1, 128]], ALU.is_gt, 0.0, 0, 1)
    iota(R("rpI"), [[1, 14], [0, 16]], 0, 0)
    iota(R("vh"), [[0, 14], [1, 16]], 0, 0)
    iota(R("num"), [[1, V + L]], 0, 0)
    ts(R("qI"), R("pI"), 15, None, ALU.bitwise_and)
    cp(R("qc"), R("qI"))
    for t in range(2):
        ts(R("pc%d" % t), R("qc"), 811.0, t - 0.375, ALU.mult, ALU.add)
        ts(R("tp%d" % t), R("qc"), -2048.0, 2048.0 * (16 + t), ALU.mult, ALU.add)
    ts(R("pk"), R("qc"), -1.0, 16.0, ALU.mult, ALU.add)
    fill(R("rneg"), 0.0)
    fill(R("rneg", 0, L, 16), -float(1 << 24))
    fill(R("zer"), 0.0)
    fill(R("rmul"), 1.0)
    fill(R("rmul", 0, L, 16), 0.0)
    ts(R("blkz"), R("blk"), 2048.0, None, ALU.mult)
    cp(R("blkf"), R("blk"))
    ts(R("chh", p=16), R("cn", p=16), float(1 << 21), -float(1 << 21), ALU.mult, ALU.add)
    ts(R("cn", p=16), R("cn", p=16), float((1 << 20) - 2048 * 120), -float(1 << 20), ALU.mult, ALU.add)
    ts(R("selk", 0, 143), R("sel1", 0, 143), 4096.0, None, ALU.mult)
    ts(R("selm", 0, 143), R("sel1", 0, 143), -2048.0, None, ALU.mult)
    ts(R("nidn"), R("idn"), -1.0, None, ALU.mult)
    ts(R("iW"), R("rowc", 0, 14), R("qc"), None, ALU.add)
    for h, (l0, l1) in enumerate(CH):
        a, b = l0 // 16, l1 // 16
        nl = l1 - l0
        ts(R("nk", a, b), R("iW", a, b), -1.0, float(4096 + 2047 + nl + l0), ALU.mult, ALU.add)
        fill(R("cb", a, b), float(BASE[h] + 2047 + nl))
    ts(R("dW"), R("iW"), float(V), None, ALU.add)
    ts(R("vW0"), R("iW"), 9.0, None, ALU.mult)

    def late_constants():
        ts(R("trid"), R("trid"), -1.0, None, ALU.mult)
        ts(R("tri"), R("vh"), R("qc"), None, ALU.is_lt)
        cp(R("rp"), R("rpI", 0, L, 16))
        cp(R("thr0"), R("thrI"))

    def sel(name, q):
        return R(name, 15 - q, 143 - q)

    def low(P, nl, last=False):
        mm(P, R("ones", 0, 128, p=1), R("rowA", 0, nl, p=1), True, False)
        mm(P, R("l16", p=16), R("rowB", 0, nl, p=16), False, False)

    def revoke(t, rv, out, banks):
        for m in range(4):
            a, b = 512 * m, 512 * m + 512
            P = R(banks[m])
            mm(P, R("idn"), R("ringS", a, b), True, False)
            if t == 1:
                mm(P, R("nidn"), R("e1", a, b), False, False)
        for m in range(4):
            a, b = 512 * m, 512 * m + 512
            ts(R("e0", a, b), R("ringS", a, b), rv, rv, ALU.is_equal, ALU.mult)
            mm(R(banks[m]), R("nidn"), R("e0", a, b), False, True)
        for m in range(4):
            a, b = 512 * m, 512 * m + 512
            if t == 0 or m % 2 == 0:
                ac(R(out, a, b), R(banks[m]))
            else:
                cp(R(out, a, b), R(banks[m]))
            if t == 1:
                dma("Y" if m % 2 else "S", T.yk[:, a:b], T[out][:, a:b], rd=[R(out, a, b)])

    def step1(t):
        zb = R("zb%d" % t)
        mm(R("PZ", 0, L), R("blkz"), zb, True, True)
        mm(R("PM", 0, L), R("idn"), zb, True, True)
        ts(R("JI"), R("PZ", 0, L), R("tp%d" % t), None, ALU.add)
        ts(R("JM"), R("JI"), 15 * 2048, None, ALU.bitwise_and)
        tt(R("YY"), R("JM"), R("nbrS", 0, 2008, 9) if t == 0 else R("BvT"), ALU.max)
        mm(R("PZ", 0, L), R("l16", p=16), R("cn", p=16), True, False)
        mm(R("PZ", 0, L), R("blkf"), R("YY"), False, True)
        scan(R("SW"), R("rneg"), R("PZ", 0, L), ALU.add, ALU.max)
        cp(R("noff"), R("SW", 15, L, 16))

    for t in range(2):
        zb, V2, vW, BIG = "zb%d" % t, "V2%d" % t, "vW%d" % t, "BIG%d" % t
        if t == 0:
            remote(T.BIG0[:, NXT:NXT + V], R("ringS", 0, V), "xr0", "xl0", prev)
            ac(R("KvT"), R("ringS", 0, 2008, 9))
            step1(0)
        ts(R("hv"), R("KvT"), 0.0, None, ALU.is_equal)
        mm(R("PK", 0, L), R("idn"), R("KvT"), True, False)
        mm(R("PK", 0, L), R("nidn"), R("hv"), False, True)
        for h, (l0, l1) in enumerate(CH):
            a, b, nl = l0 // 16, l1 // 16, l1 - l0
            no = R("noff", a, b)
            cp(R("Bn", l0, l1), X("nbrS", 0, V, no), off=[no])
            ac(R(BIG, BASE[h], BASE[h] + nl), X("ringS", 0, V, no), off=[no])

        def gk(h, a, b):
            l0, l1 = CH[h]
            lo = BASE[h] + (l1 - l0) + 16 * (a - l0)
            o = R("Bn", a, b)
            ac(R(BIG, lo, lo + 16 * (b - a)), X("ringS", 0, V, o), off=[o])

        gk(0, 0, 64)
        gk(0, 64, 128)
        gk(1, 128, 224)
        for h, (l0, l1) in enumerate(CH):
            nl = l1 - l0
            ts(R("hn", l0, l1), R(BIG, BASE[h], BASE[h] + nl), 0.0, None, ALU.is_equal)
            P = R("PK", L + l0, L + l1)
            mm(P, R("idn"), R(BIG, BASE[h], BASE[h] + nl), True, False)
            mm(P, R("nidn"), R("hn", l0, l1), False, True)
        for h, (l0, l1) in enumerate(CH):
            tt(R("E3", l0, l1), R("PK", l0, l1), R(BIG, BASE[h], BASE[h] + l1 - l0), ALU.is_equal)
        if t == 0:
            late_constants()

        def compare(h, which, parts):
            l0, l1 = CH[h]
            nl, nc = l1 - l0, (l1 - l0) // 16
            En, ko = ("E1", 0) if which == 0 else ("E2", L)
            for a, b in parts:
                lo = BASE[h] + nl + 16 * (a - l0)
                for k in range(16):
                    tt(E3d(En, a, b, k=k), R("PK", ko + a, ko + b), R(BIG, lo + k, lo + 16 * (b - a), 16), ALU.is_equal)
            if which == 0:
                P = R("PC%d" % h, 2 * nl, 2 * nl + nc)
                for q in range(16):
                    mm(P, sel("sel1", q), R("E3", l0 + q, l1, 16), q == 0, q == 15)
            P = R("PC%d" % h, which * nl, (which + 1) * nl)
            low(P, nl)
            for q in range(16):
                mm(P, sel("selk", q), E3d(En, l0, l1, q=q), False, q == 15)

        def tail(h):
            l0, l1 = CH[h]
            a, b, nl, nc = l0 // 16, l1 // 16, l1 - l0, (l1 - l0) // 16
            PC = "PC%d" % h
            cp(R("M2", 0, nl), R(PC, nl, 2 * nl))
            ts(R("xn", a, b), R(PC, 2 * nl, 2 * nl + nc), 2.0, float(1 << 18), ALU.is_ge, ALU.mult)
            tt(R("MM", 0, nl), R(PC, 0, nl), R("M2", 0, nl), ALU.min)
            tt(R("xn", a, b), R("xn", a, b), R("nk", a, b), ALU.add)
            scan(R("SK", l0, l1), R("rneg", 0, nl), R("MM", 0, nl), ALU.add, ALU.max)
            tt(R("KI", a, b), R("SK", l0 + 15, l1, 16), R("xn", a, b), ALU.max)
            ts(R("KA", a, b), R("KI", a, b), 4095, None, ALU.bitwise_and)
            po = R("posU", a, b)
            ts(po, R("KA", a, b), -1.0, float(2047 + nl), ALU.mult, ALU.add)
            w = X(BIG, BASE[h], BASE[h] + 17 * nl, po)
            tt(R("PR", 0, nl), w, R(V2, l0, l1), ALU.mult, off=[po])
            ac(R("KwT", l0, l1), w, off=[po])
            ts(R("PI", 0, nl), R("PR", 0, nl), 0.25, R("pc%d" % t), ALU.mult, ALU.add)
            ts(R("PJ", 0, nl), R("PI", 0, nl), 4095, None, ALU.bitwise_and)
            cp(R("PL", l0, l1), R("PJ", 0, nl))

        def gx(h):
            l0, l1 = CH[h]
            o = R("PL", l0, l1)
            ac(R("XC%d" % h), X("matS", 0, 4096, o), off=[o])

        def dsub(h, m):
            l0, l1 = CH[h]
            nl = l1 - l0
            bank = ("PC0", "PK", "PC1")[(4 * h + m) % 3]
            for p in range(4 * m, 4 * m + 4):
                P = R(bank, (p & 3) * 128, (p & 3) * 128 + nl)
                mm(P, R("nidn"), R(zb, l0, l1), True, False)
                mm(P, R("idn"), R("XC%d" % h, p, 16 * nl, 16), False, True)
            for p in range(4 * m, 4 * m + 4):
                ac(E3d("DD", l0, l1, k=p), R(bank, (p & 3) * 128, (p & 3) * 128 + nl), AF.Abs)

        def dW(h, m):
            l0, l1 = CH[h]
            P = R("PD%d" % h, 0, l1 - l0)
            if m == 0:
                low(P, l1 - l0)
            for q in range(4 * m, 4 * m + 4):
                mm(P, sel("selm", q), E3d("DD", l0, l1, q=q), False, q == 15)

        def dA(h, m):
            l0, l1 = CH[h]
            for p in range(4 * m, 4 * m + 4):
                mm(R("PA", l0, l1), sel("sel1", p), E3d("DD", l0, l1, k=p), p == 0, p == 15)

        def best(h):
            l0, l1 = CH[h]
            a, b, nl = l0 // 16, l1 // 16, l1 - l0
            scan(R("SD", l0, l1), R("rneg", 0, nl), R("PD%d" % h, 0, nl), ALU.add, ALU.max)
            cp(R("DI", a, b), R("SD", l0 + 15, l1, 16))
            ts(R("DA", a, b), R("DI", a, b), 2047, None, ALU.bitwise_and)
            po = R("pxU", a, b)
            ts(po, R("DA", a, b), -1.0, 2047.0, ALU.mult, ALU.add)
            tt(R("ZS", 0, nl), X("XC%d" % h, 0, 16 * nl, po), R(zb, l0, l1), ALU.add, off=[po])
            ts(R("ZI", 0, nl), R("ZS", 0, nl), 0.5, -0.25, ALU.mult, ALU.add)
            cp(R("zb1" if t == 0 else "zf", l0, l1), R("ZI", 0, nl))

        compare(0, 0, [(0, 64), (64, 128)])
        compare(0, 1, [(0, 128)])
        compare(1, 0, [(128, 224)])
        tail(0)
        gx(0)
        compare(1, 1, [(128, 224)])
        tail(1)
        gx(1)
        ts(R("FF"), R("KI"), 8192.0, None, ALU.is_lt)
        emit("V", lambda: g.vector.tensor_tensor_scan(T.Finc[:, :], T.FF[:, :], T.zer[:, 0:14], 0.0, ALU.add, ALU.add), [R("FF"), R("zer", 0, 14)], [R("Finc")])
        mm(R("PZ", 224, 238), R("blk"), R("Finc"), True, False)
        mm(R("PZ", 224, 238), R("trid"), R("FF"), False, True)
        if t == 0:
            mm(R("PZ", 240, 254), R("ones", 0, 128), R("FF"), True, True)
        tt(R("HZ"), R("PM", 0, L), R("KwT"), ALU.mult)
        mm(R("PZ", 0, L), R("l16", p=16), R("chh", p=16), True, False)
        mm(R("PZ", 0, L), R("blkf"), R("HZ"), False, True)
        ts(R("nd"), R("KI"), float(1 << 18), None, ALU.is_lt)
        tt(R("bb"), R("nd"), R("FF"), ALU.subtract)
        if t == 0:
            cp(R("nW"), R("SW", 15, L, 16))
            ts(R("KK"), R("KA"), 15, None, ALU.bitwise_and)
            cp(R("BnF"), R("Bn"))
            ts(R("th"), R("KK"), 1.0, None, ALU.add)
            tt(R("th"), R("th"), R("bb"), ALU.mult)
            cp(R("cdU"), R("th"))
            cp(R("cdR"), X("num", 0, 32, R("cdU")), off=[R("cdU")])
            ts(R("mk"), R("cdR"), R("pk"), None, ALU.is_equal)
            tt(R("YW"), R("mk"), R("BnF"), ALU.mult)
            mm(R("PM", L, 2 * L), R("l16", p=16), R("chh", p=16), True, False)
            mm(R("PM", L, 2 * L), R("blkf"), R("YW"), False, True)
        scan(R("SH"), R("rneg"), R("PZ", 0, L), ALU.add, ALU.max)
        ts(R("srv"), R("PZ", 224, 238), 48.0, None, ALU.is_le)
        if t == 0:
            red(R("fc"), R("PZ", 240, 254), ALU.add)
        cp(R("HI"), R("SH", 15, L, 16))
        ts(R("HJ"), R("HI"), V - 1, None, ALU.bitwise_and)
        ts(R("ths"), R("bb"), -8192.0, float(NXT), ALU.mult, ALU.add)
        tt(R("sp"), R("cb"), R("KA"), ALU.subtract)
        tt(R("ths"), R("ths"), R("HJ"), ALU.add)
        tt(R("sp"), R("sp"), R("ths"), ALU.max)
        cp(R("spU"), R("sp"))
        landed(BIG, NXT, NXT + V, "xr%d" % t, "xl%d" % t, nxt)
        if t == 0:
            ts(R("nb"), R("bb"), -1.0, 1.0, ALU.mult, ALU.add)
            scan(R("SV"), R("rneg"), R("PM", L, 2 * L), ALU.add, ALU.max)
            tt(R("taB"), R("nb"), R("dW"), ALU.mult)
            tt(R("thn"), R("nb"), R("nW"), ALU.mult)
            tt(R("oB2"), R("taB"), R("vW0"), ALU.max)
            tt(R("vW1"), R("SV", 15, L, 16), R("thn"), ALU.add)
            cp(R("oBU"), R("oB2"))
            cp(R("voff"), R("vW1"))
        ac(R("NZ"), R("KwT"), AF.Sign)
        dsub(0, 0)
        dsub(0, 1)
        ac(R("SRC"), X(BIG, 0, NXT + V, R("spU")), off=[R("spU")])
        if t == 0:
            ac(R("wR"), X("num", 0, V, R("voff")), off=[R("voff")])
        tt(R("N1"), R("NZ"), R("ramp"), ALU.mult)
        dsub(0, 2)
        dA(0, 0)
        dsub(0, 3)
        dA(0, 1)
        mm(R("PZ", 256, 256 + L), R("idn"), R("N1"), True, False)
        mm(R("PZ", 256, 256 + L), R("idn"), R("KwT"), False, True)
        tt(R("srv"), R("srv"), R("FF"), ALU.mult)
        tt(R("srv"), R("srv"), R("bb"), ALU.add)
        ts(R("ta"), R("srv"), -1.0, 1.0, ALU.mult, ALU.add)
        tt(R("ta"), R("ta"), R("dW"), ALU.mult)
        tt(R("oKf"), R("ta"), R(vW), ALU.max)
        if t == 0:
            tt(R("Bm"), R("nbrS", 0, 2008, 9), R("JM"), ALU.min)
            cp(R("oKU", 0, 14), R("oKf"))
            tt(R("FP"), R("hv"), R("SRC"), ALU.mult)
            tt(R("Bs"), R("wR"), R("JM"), ALU.subtract)
            tt(R("Bx"), R("Bm"), R("Bs"), ALU.max)
            cp(X("nbrS", 0, V + L, R("oBU")), R("Bx"), off=[R("oBU")])
            tt(X("ringS", 0, V + L, R("oKU", 0, 14)), R("KvT"), R("FP"), ALU.add, off=[R("oKU", 0, 14)])
            cp(R("BvT"), X("nbrS", 0, V, R("voff")), off=[R("voff")])
            cp(R("fi"), R("fc"))
            ts(R("fj"), R("fi"), 15, None, ALU.bitwise_and)
            tt(R("thr1"), R("fj"), R("thr0"), ALU.add)
        else:
            cp(R("oBU"), R("oKf"))
            cp(R("va"), X("num", 0, V + L, R("oBU")), off=[R("oBU")])
            cp(R("vWp", 0, 14), R(vW))
            cp(R("vh"), X("vWp", 0, 14, R("rp")), off=[R("rp")])
            tt(R("eq"), R("va"), R("vh"), ALU.is_equal)
            tt(R("eq"), R("eq"), R("tri"), ALU.mult)
            scan(R("SE"), R("rmul"), R("eq"), ALU.mult, ALU.add)
            ts(R("ta"), R("SE", 15, L, 16), 0.5, None, ALU.is_ge)
            tt(R("FP"), R("hv"), R("SRC"), ALU.mult)
            tt(R("ta"), R("ta"), R("dW"), ALU.mult)
            tt(R("oKf"), R("oKf"), R("ta"), ALU.max)
            cp(R("oKU", 0, 28, 2), R("oKf"))
            for c in range(13, -1, -1):
                o = R("oKU", 2 * c, 2 * c + 1)
                tt(X("ringS", 0, V + L, o), R("KvT", 16 * c, 16 * c + 16), R("FP", 16 * c, 16 * c + 16), ALU.add, off=[o])
            landed("come", 0, 1, "rr", "rl", prev)
            cm = R("come", 0, 1)
            for m in range(4):
                a, b = 512 * m, 512 * m + 512
                ts(R("e1", a, b), R("ringS", a, b), cm, cm, ALU.is_equal, ALU.mult)
        dA(0, 2)
        for m in range(4):
            dsub(1, m)
            if m == 0:
                dA(0, 3)
            dW(0, m)
            if t == 0 and m == 2:
                ac(R("V21"), R("wR"), AF.Identity, bias=1.0, scale=2.0)
        for m in range(4):
            dA(1, m)
        for m in range(4):
            dW(1, m)
        best(0)
        ts(R("cap"), R("PA", 0, L), R("thr%d" % t), None, ALU.is_lt)
        tt(R("com"), R("PZ", 256, 256 + L), R("cap"), ALU.mult)
        if t == 0:
            best(1)
        red(R("rvc"), R("com"), ALU.max)
        cp(R("rvi"), R("rvc"))
        ts(R("rvj"), R("rvi"), 255, None, ALU.bitwise_and)
        if t == 0:
            cp(R("rv0", 0, 1), R("rvj"))
            step1(1)
            remote(T.come[:, 0:1], R("rv0", 0, 1), "rr", "rl", nxt)
            revoke(0, R("rv0", 0, 1), "ringS", ("PC0", "PC1", "PK", "PD0"))
            remote(T.BIG1[:, NXT:NXT + V], R("ringS", 0, V), "xr1", "xl1", prev)
            ac(R("KvT"), X("ringS", 0, V, R("voff")), off=[R("voff")])
        else:
            cp(R("rv1", 0, 1), R("rvj"))
            tt(R("tmpc"), R("rv1", 0, 1), cm, ALU.not_equal)
            tt(R("rv1", 1, 2), R("rv1", 0, 1), R("tmpc"), ALU.mult)
            revoke(1, R("rv1", 1, 2), "ykS", ("PC0", "PC1", "PK", "PA"))
            best(1)
            dma("Y", T.yz[:, :], T.zf[:, :], rd=[R("zf")])
    if not PLAN:
        PLAN.extend(order())
    for i in PLAN:
        issue(*ops[i])
    for s, c in total.items():
        if known["Y"].get(s, 0) < c:
            g.sync.wait_ge(T.sem[s], c)
